import numpy as np
import ml_dtypes


def mxq(x, axis, fmt="e4m3"):
    dtype, down = {"e4m3": (ml_dtypes.float8_e4m3fn, 7), "e5m2": (ml_dtypes.float8_e5m2, 14)}[fmt]
    v = np.moveaxis(np.asarray(x, np.float32).astype(ml_dtypes.bfloat16).astype(np.float64), axis, -1)
    blocks = v.reshape(v.shape[:-1] + (-1, 32))
    amax = np.abs(blocks).max(-1, keepdims=True)
    byte = np.maximum(np.where(amax > 0, np.frexp(amax)[1] - 1 + 127, 0) - down, 1)
    scale = np.exp2(byte - 127.0)
    codes = (blocks / scale).astype(np.float32).astype(dtype).astype(np.float64)
    return np.moveaxis((codes * scale).reshape(v.shape), -1, axis)


WIDE = False


def mx_kscale(k):
    if not WIDE:
        return np.ones(k)
    levels = np.array([30, -30])
    if k % 512:
        return np.exp2(np.random.permutation(np.resize(levels, k // 32))).repeat(32)
    a = np.empty((k // 512, 16))
    for p in range(k // 512):
        a[p, :8] = np.random.permutation(np.resize(levels, 8))
        for g in range(8):
            far = levels[np.abs(levels - a[p, g]) >= 10]
            a[p, g + 8] = far[np.random.randint(len(far))]
    return np.exp2(a.ravel()).repeat(32)


BF16 = ml_dtypes.bfloat16


def bf(x):
    return np.asarray(x, np.float32).astype(BF16)


def f64(x):
    return np.asarray(x).astype(np.float64)


E2M1 = np.array([0.0, 0.5, 1.0, 1.5, 2.0, 3.0, 4.0, 6.0, -0.0, -0.5, -1.0, -1.5, -2.0, -3.0, -4.0, -6.0])


def pack_weight(w, fmt):
    k, n = w.shape
    w = f64(bf(w)).reshape(k // 32, 32, n)
    amax = np.abs(w).max(1)
    if fmt in ("e4m3", "e5m2"):
        byte = np.frexp(amax)[1] - 1 + 127 - (7 if fmt == "e4m3" else 14)
    else:
        mant, ex = np.frexp(amax / 6.0)
        byte = np.where(mant > 0.5, ex, ex - 1) + 127
    byte = np.clip(np.where(amax > 0, byte, 1), 1, 254)
    scaled = (w * np.exp2(127.0 - byte)[:, None, :]).reshape(k, n).astype(np.float32)
    by_word = np.ascontiguousarray(scaled.reshape(k // 512, 128, 4, n).transpose(0, 1, 3, 2))
    if fmt in ("e4m3", "e5m2"):
        words = by_word.astype(ml_dtypes.float8_e4m3fn if fmt == "e4m3" else ml_dtypes.float8_e5m2).view(np.uint8)
    else:
        c = by_word.astype(ml_dtypes.float4_e2m1fn).view(np.uint8) & 0xF
        words = c[..., 0::2] | (c[..., 1::2] << 4)
    return np.ascontiguousarray(words), np.ascontiguousarray(byte.astype(np.uint8).reshape(k // 512, 16, n))


def unpack_weight(words, scales, fmt):
    g, p, n, _ = words.shape
    if fmt in ("e4m3", "e5m2"):
        vals = np.ascontiguousarray(words).view(ml_dtypes.float8_e4m3fn if fmt == "e4m3" else ml_dtypes.float8_e5m2).astype(np.float64)
    else:
        nib = np.empty((g, p, n, 4), np.uint8)
        nib[..., 0::2] = words & 0xF
        nib[..., 1::2] = words >> 4
        vals = E2M1[nib]
    vals = vals * np.repeat(np.exp2(scales.astype(np.float64) - 127.0), 8, axis=1)[..., None]
    return vals.transpose(0, 1, 3, 2).reshape(g * 512, n)


N = 1024


def setup_inputs():
    s, u = mx_kscale(N), mx_kscale(N)
    a = np.random.standard_normal((N, N))
    b = np.random.standard_normal((N, N))
    c = np.random.standard_normal((N, N))
    h = np.random.standard_normal((N, N))
    a, b, c, h = [(x + x.T) / np.sqrt(2) for x in (a, b, c, h)]
    e = np.random.uniform(0.0, 1.5, N)
    G = a * np.abs(a) / np.sqrt(3)
    G_words, G_scales = pack_weight(G * s[:, None], "e5m2")
    return {"g_words": G_words,
            "g_scales": G_scales,
            "d": bf(b / np.sqrt(N) / s[:, None]),
            "f": bf(c * u),
            "r": bf(h / np.sqrt(N) / u[:, None]),
            "w": bf(1 / (0.5 + np.abs(e[:, None] - e)))}


def reference(g_words, g_scales, d, f, r, w):
    G = unpack_weight(g_words, g_scales, "e5m2")
    gd = G.T @ mxq(f64(d), 0, "e4m3")
    fr = mxq(f64(f), 1, "e4m3") @ mxq(f64(r), 0, "e4m3")
    T = gd + fr
    return f64(w) * (T - T.T)

@@ -1,0 +1,368 @@
+from contextlib import ExitStack
+
+import concourse.mybir as mybir
+from concourse.masks import make_identity
+
+N = 1024
+FLOPS = 4 * N * N * N
+
+F32 = mybir.dt.float32
+BF16 = mybir.dt.bfloat16
+I32 = mybir.dt.int32
+U32 = mybir.dt.uint32
+U8 = mybir.dt.uint8
+E4M3 = mybir.dt.float8_e4m3fn_x4
+E5M2 = mybir.dt.float8_e5m2_x4
+MULT = mybir.AluOpType.mult
+SUB = mybir.AluOpType.subtract
+
+P = 128
+PACK = 4
+KP = 512
+H = 512
+TILES = 4
+
+
+def tile_commutator_directional_derivative_e4_kernel(tc, g_words, g_scales, d, f, r, w, out):
+    nc = tc.nc
+    src = {"d": d, "r": r}
+    with ExitStack() as ctx:
+        sb = ctx.enter_context(tc.tile_pool(name="sb", bufs=1))
+        ps = ctx.enter_context(tc.psum_pool(name="ps", bufs=1))
+        bank = [ps.tile([P, H], F32, name="bank%d" % k) for k in range(8)]
+        ident = sb.tile([P, P], F32, name="ident")
+        pieces = [(h, g) for h in range(2) for g in range(2)]
+        raw = {(x, h, g): sb.tile([P, PACK, H], BF16, name="raw_%s%d%d" % (x, h, g)) for x in "dr" for h, g in pieces}
+        grouped = {(x, h, g): sb.tile([P, H, PACK], BF16, name="grp_%s%d%d" % (x, h, g), align_bytes=64) for x in "dr" for h, g in pieces}
+        f_grouped = [sb.tile([P, 2, H, PACK], BF16, name="grp_f%d" % h, align_bytes=64) for h in range(2)]
+        codes = {(x, h, g): sb.tile([P, H], U32, name="codes_%s%d%d" % (x, h, g), align_bytes=64) for x in "drf" for h, g in pieces}
+        scales = {(x, h, g): sb.tile([P, H], U8, name="scales_%s%d%d" % (x, h, g), align_bytes=64) for x in "drf" for h, g in pieces}
+        g_codes = [sb.tile([P, 2, H], U32, name="g_codes%d" % h, align_bytes=64) for h in range(2)]
+        warm = sb.tile([P, 8], F32, name="warm")
+        g_plane = sb.tile([P, 2, N], U8, name="g_plane", align_bytes=64)
+        f_raw = [sb.tile([P, N], BF16, name="f_raw%d" % m) for m in range(2)]
+        f_raw2 = [sb.tile([P, 2, N], BF16, name="f_pair%d" % m) for m in range(3)]
+        w_sb = [sb.tile([P, TILES, N], BF16, name="w_sb%d" % h) for h in range(2)]
+        t_sb = {q: sb.tile([P, TILES, H], F32, name="t_sb%s" % q) for q in ("00", "01", "11")}
+        a_sb = {q: sb.tile([P, TILES, H], F32, name="a_sb%s" % q) for q in ("00", "11")}
+        o_sb = {q: sb.tile([P, TILES, H], F32, name="o_sb%s" % q) for q in ("00", "01", "10", "11")}
+
+        def f_rows(m):
+            return f_raw[m][:] if m < 2 else f_raw2[m // 2 - 1][:, m % 2, :]
+
+        def load_f(m):
+            if m < 2:
+                nc.sync.dma_start(out=f_raw[m][:], in_=f[m * P:(m + 1) * P, :])
+            else:
+                nc.sync.dma_start(out=f_raw2[m // 2 - 1][:], in_=f[m * P:(m + 2) * P, :].rearrange("(a p) l -> p a l", p=P))
+
+        def load_x(x, h, g, c0=0, c1=H):
+            nc.sync.dma_start(out=raw[x, h, g][:, :, c0:c1], in_=src[x][g * KP:(g + 1) * KP, h * H + c0:h * H + c1].rearrange("(p t) c -> p t c", t=PACK))
+
+        def load_g(h, g0, g1):
+            words = g_words[g0:g1].rearrange("g p n t -> p g (n t)")[:, :, h * H * PACK:(h + 1) * H * PACK]
+            nc.sync.dma_start(out=g_codes[h][:, g0:g1, :].bitcast(I32), in_=words.bitcast(I32))
+
+        def load_g_scales():
+            nc.vector.memset(g_plane[:].rearrange("p g n -> p (g n)").bitcast(I32), 0)
+            for q in range(4):
+                nc.scalar.dma_start(out=g_plane[32 * q:32 * q + 4, :, :].bitcast(I32), in_=g_scales[:, 4 * q:4 * q + 4, :].rearrange("g r n -> r g n").bitcast(I32))
+            nc.vector.memset(warm[:, 0:1], 0.0)
+            nc.scalar.mul(out=warm[:, 1:2], in_=warm[:, 0:1], mul=-1.0)
+
+        def load_w(h):
+            nc.sync.dma_start(out=w_sb[h][:], in_=w[h * H:(h + 1) * H, :].rearrange("(a p) j -> p a j", p=P))
+
+        def turn_f(m, k0):
+            words = f_rows(m).bitcast(F32)
+            for g in range(2):
+                for u in range(2):
+                    k = 2 * g + u
+                    nc.tensor.transpose(bank[k0][:, k * P:(k + 1) * P], words[:, 256 * g + u:256 * (g + 1):2], ident[:])
+
+        def unload_f(m, k0):
+            h, a = divmod(m, TILES)
+            dst = f_grouped[h][:, :, a * P:(a + 1) * P, :].bitcast(F32)
+            nc.scalar.copy(out=dst, in_=bank[k0][:].rearrange("p (g u i) -> p g i u", g=2, u=2))
+
+        def group(eng, x, h, g, c0, c1):
+            dst = grouped[x, h, g][:, c0:c1, :].rearrange("p (c i) t -> p c t i", i=4)
+            s = raw[x, h, g][:, :, c0:c1].rearrange("p t (c i) -> p c t i", i=4)
+            if eng == "V":
+                if h == 0:
+                    nc.vector.tensor_scalar_mul(out=dst, in0=s, scalar1=-1.0)
+                else:
+                    nc.vector.tensor_copy(out=dst, in_=s)
+            elif h == 0:
+                nc.scalar.mul(out=dst, in_=s, mul=-1.0)
+            else:
+                nc.scalar.copy(out=dst, in_=s)
+
+        def quant(x, h, g, c0=0, c1=H):
+            values = f_grouped[h][:, g, c0:c1, :] if x == "f" else grouped[x, h, g][:, c0:c1, :]
+            nc.vector.quantize_mx(out=codes[x, h, g][:, c0:c1].bitcast(E4M3), scales=scales[x, h, g][:, c0:c1],
+                                  in_=values.rearrange("p c t -> p (c t)"))
+
+        def operand(x, h, g, c0, c1):
+            if x == "G":
+                return g_codes[h][:, g, c0:c1].bitcast(E5M2), g_plane[:, g, h * H + c0:h * H + c1]
+            return codes[x, h, g][:, c0:c1].bitcast(E4M3), scales[x, h, g][:, c0:c1]
+
+        def mx(k, a, stat, mov, g, start=False, stop=False):
+            lhs, lhs_scale = operand(stat[0], int(stat[1]), g, a * P, (a + 1) * P)
+            rhs, rhs_scale = operand(mov[0], int(mov[1]), g, 0, H)
+            nc.tensor.matmul_mx(out=bank[k][:], lhsT=lhs, lhsT_scale=lhs_scale, rhs=rhs, rhs_scale=rhs_scale, start=start, stop=stop)
+
+        def mx4(k0, stat, mov, g, start=False, stop=False):
+            for a in range(TILES):
+                mx(k0 + a, a, stat, mov, g, start, stop)
+
+        def unload_t(q, k, a):
+            if q == "01":
+                nc.scalar.mul(out=t_sb[q][:, a, :], in_=bank[k][:], mul=-1.0)
+            else:
+                nc.scalar.copy(out=t_sb[q][:, a, :], in_=bank[k][:])
+
+        def turn(k, slot, q, a, b):
+            nc.tensor.transpose(bank[k][:, slot * P:(slot + 1) * P], t_sb[q][:, a, b * P:(b + 1) * P], ident[:])
+
+        def turn_box(q, k, rows, cols):
+            slot = 0
+            for a in range(*rows):
+                for b in range(*cols):
+                    turn(k, slot, q, b, a)
+                    slot += 1
+
+        def turn_row(q, k, a, n):
+            turn_box(q, k, (a, a + 1), (0, n))
+
+        def turn_col(q, k, b):
+            turn_box(q, k, (0, 4), (b, b + 1))
+
+        def blocks(tile, rows, cols):
+            return tile[:, rows[0]:rows[1], cols[0] * P:cols[1] * P]
+
+        def bank_as(k, rows, cols, s0=0):
+            n = (rows[1] - rows[0]) * (cols[1] - cols[0])
+            return bank[k][:, s0 * P:(s0 + n) * P].rearrange("p (a c) -> p a c", a=rows[1] - rows[0])
+
+        def sub(q, k, rows, cols, s0=0):
+            t, tt = blocks(t_sb[q], rows, cols), bank_as(k, rows, cols, s0)
+            nc.vector.tensor_tensor(out=blocks(a_sb[q], rows, cols), in0=t, in1=tt, op=SUB)
+
+        def w_blocks(q, rows, cols):
+            c = int(q[1]) * TILES
+            return blocks(w_sb[int(q[0])], rows, (cols[0] + c, cols[1] + c))
+
+        def weigh(q, rows, cols, k=None, eng=None):
+            a = blocks(a_sb[q], rows, cols) if k is None else bank_as(k, rows, cols)
+            (eng or nc.vector).tensor_tensor(out=blocks(o_sb[q], rows, cols), in0=a, in1=w_blocks(q, rows, cols), op=MULT)
+
+        def store(q, rows, cols):
+            r0, c0 = int(q[0]) * H, int(q[1]) * H
+            dst = out[r0 + rows[0] * P:r0 + rows[1] * P, c0 + cols[0] * P:c0 + cols[1] * P].rearrange("(a p) j -> p a j", p=P)
+            nc.sync.dma_start(out=dst, in_=blocks(o_sb[q], rows, cols))
+
+        with tc.manual_schedule():
+            make_identity(nc, ident[:])
+            load_f(1)
+            load_g_scales()
+            turn_f(1, 5)
+            load_x("d", 0, 1)
+            group("S", "d", 0, 1, 128, 256)
+            load_x("d", 0, 0, 0, 256)
+            load_f(2)
+            load_g(0, 1, 2)
+            group("S", "d", 0, 1, 448, 512)
+            turn_f(2, 6)
+            group("V", "d", 0, 1, 0, 128)
+            quant("d", 0, 1, 0, 256)
+            turn_f(3, 7)
+            load_f(0)
+            load_x("r", 0, 0)
+            group("V", "d", 0, 1, 256, 448)
+            group("V", "d", 0, 0, 0, 128)
+            quant("d", 0, 1, 256, 512)
+            turn_f(0, 4)
+            mx(2, 2, "d0", "G0", 1, start=True)
+            mx(3, 3, "d0", "G0", 1, start=True)
+            load_f(6)
+            load_f(4)
+            group("S", "d", 0, 0, 128, 256)
+            unload_f(2, 6)
+            load_x("r", 0, 1)
+            unload_f(3, 7)
+            unload_f(1, 5)
+            quant("f", 0, 1, 256, 512)
+            group("V", "r", 0, 0, 256, 512)
+            quant("f", 0, 0, 256, 512)
+            mx(1, 1, "d0", "G0", 1, start=True)
+            quant("r", 0, 0, 256, 512)
+            unload_f(0, 4)
+            group("V", "r", 0, 0, 0, 256)
+            turn_f(7, 7)
+            quant("f", 0, 0, 0, 256)
+            quant("f", 0, 1, 0, 256)
+            turn_f(6, 6)
+            quant("r", 0, 0, 0, 256)
+            group("V", "r", 0, 1, 0, 256)
+            quant("d", 0, 0, 0, 256)
+            unload_f(7, 7)
+            unload_f(6, 6)
+            turn_f(5, 5)
+            turn_f(4, 4)
+            mx(2, 2, "r0", "f0", 0)
+            quant("f", 1, 1, 256, 512)
+            unload_f(5, 5)
+            unload_f(4, 4)
+            quant("f", 1, 1, 0, 256)
+            load_g(1, 0, 2)
+            load_g(0, 0, 1)
+            load_x("d", 0, 0, 256, 512)
+            load_x("r", 1, 0)
+            mx(3, 3, "r0", "f0", 0)
+            mx(0, 0, "r0", "f0", 0, start=True)
+            mx(1, 1, "r0", "f0", 0)
+            load_x("d", 1, 0)
+            group("S", "r", 0, 1, 256, 512)
+            load_x("d", 1, 1)
+            group("S", "d", 0, 0, 352, 512)
+            group("S", "r", 1, 0, 160, 512)
+            group("S", "d", 1, 0, 448, 512)
+            mx(0, 0, "d0", "G0", 1)
+            quant("r", 0, 1, 0, 256)
+            mx(7, 3, "d0", "G1", 1, start=True)
+            mx(5, 1, "d0", "G1", 0, start=True)
+            mx(4, 0, "d0", "G1", 1, start=True)
+            group("V", "d", 0, 0, 256, 352)
+            mx(5, 1, "d0", "G1", 1)
+            load_x("r", 1, 1)
+            mx(0, 0, "d0", "G0", 0)
+            mx(5, 1, "r0", "f1", 1)
+            load_w(1)
+            load_w(0)
+            quant("f", 1, 0, 0, 256)
+            mx(1, 1, "d0", "G0", 0)
+            mx(4, 0, "d0", "G1", 0)
+            quant("f", 1, 0, 256, 512)
+            quant("d", 0, 0, 256, 512)
+            mx(4, 0, "r0", "f1", 1)
+            mx(4, 0, "r0", "f1", 0)
+            mx(0, 0, "r0", "f0", 1, stop=True)
+            mx(6, 2, "d0", "G1", 0, start=True)
+            mx(1, 1, "r0", "f0", 1, stop=True)
+            unload_t("00", 1, 1)
+            group("V", "r", 1, 0, 0, 160)
+            quant("r", 0, 1, 256, 512)
+            group("V", "d", 1, 0, 0, 448)
+            quant("r", 1, 0, 0, 512)
+            unload_t("00", 0, 0)
+            mx(2, 2, "d0", "G0", 0)
+            mx(7, 3, "d0", "G1", 0)
+            mx(5, 1, "r0", "f1", 0)
+            mx(3, 3, "r0", "f0", 1)
+            mx(2, 2, "r0", "f0", 1, stop=True)
+            mx(7, 3, "r0", "f1", 0)
+            mx(6, 2, "r0", "f1", 1)
+            mx(3, 3, "d0", "G0", 0, stop=True)
+            quant("d", 1, 0, 0, 512)
+            group("V", "d", 1, 1, 0, 160)
+            unload_t("00", 2, 2)
+            unload_t("00", 3, 3)
+            mx(6, 2, "d0", "G1", 1)
+            mx(6, 2, "f0", "r1", 0)
+            mx(4, 0, "G0", "d1", 0)
+            mx(7, 3, "f0", "r1", 0)
+            group("V", "r", 1, 1, 0, 384)
+            mx(7, 3, "G0", "d1", 0)
+            turn_row("00", 0, 0, 4)
+            turn_row("00", 1, 1, 4)
+            turn_row("00", 3, 3, 4)
+            turn_row("00", 2, 2, 4)
+            mx(4, 0, "f0", "r1", 0)
+            mx(6, 2, "r0", "f1", 0)
+            mx(6, 2, "G0", "d1", 0)
+            group("S", "r", 1, 1, 384, 512)
+            group("S", "d", 1, 1, 160, 512)
+            quant("r", 1, 1, 0, 512)
+            sub("00", 1, (1, 2), (0, 4))
+            sub("00", 3, (3, 4), (0, 4))
+            quant("d", 1, 1, 0, 512)
+            mx(1, 1, "f1", "r1", 1, start=True)
+            mx(4, 0, "f0", "r1", 1)
+            mx(5, 1, "G0", "d1", 0)
+            mx(7, 3, "r0", "f1", 1)
+            sub("00", 0, (0, 1), (0, 4))
+            weigh("00", (3, 4), (0, 4))
+            weigh("00", (1, 2), (0, 4))
+            sub("00", 2, (2, 3), (0, 4))
+            mx(7, 3, "f0", "r1", 1)
+            mx(7, 3, "G0", "d1", 1, stop=True)
+            mx(4, 0, "G0", "d1", 1, stop=True)
+            weigh("00", (0, 1), (0, 4))
+            mx(6, 2, "f0", "r1", 1)
+            mx(5, 1, "G0", "d1", 1)
+            unload_t("01", 4, 0)
+            mx(6, 2, "G0", "d1", 1, stop=True)
+            mx(0, 0, "G1", "d1", 0, start=True)
+            unload_t("01", 7, 3)
+            mx(5, 1, "f0", "r1", 1)
+            mx(5, 1, "f0", "r1", 0, stop=True)
+            mx(0, 0, "f1", "r1", 1)
+            mx(1, 1, "G1", "d1", 0)
+            weigh("01", (0, 1), (0, 4), k=4)
+            store("00", (0, 2), (0, 4))
+            mx(0, 0, "f1", "r1", 0)
+            unload_t("01", 5, 1)
+            unload_t("01", 6, 2)
+            mx(0, 0, "G1", "d1", 1, stop=True)
+            mx(2, 2, "G1", "d1", 0, start=True)
+            mx(1, 1, "G1", "d1", 1)
+            unload_t("11", 0, 0)
+            mx(1, 1, "f1", "r1", 0, stop=True)
+            unload_t("11", 1, 1)
+            weigh("01", (3, 4), (0, 4), k=7)
+            turn_col("01", 7, 3)
+            turn_col("01", 4, 0)
+            weigh("01", (1, 2), (0, 4), k=5)
+            weigh("01", (2, 3), (0, 4), k=6)
+            weigh("00", (2, 3), (0, 4))
+            weigh("10", (0, 4), (0, 1), k=4)
+            turn_col("01", 5, 1)
+            weigh("10", (0, 4), (1, 2), k=5)
+            turn_col("01", 6, 2)
+            turn_box("11", 0, (0, 2), (0, 2))
+            mx(2, 2, "G1", "d1", 1)
+            mx(2, 2, "f1", "r1", 1)
+            store("01", (2, 4), (0, 4))
+            mx(2, 2, "f1", "r1", 0, stop=True)
+            mx(3, 3, "f1", "r1", 1, start=True)
+            mx(3, 3, "G1", "d1", 1)
+            mx(3, 3, "f1", "r1", 0)
+            weigh("10", (0, 4), (3, 4), k=7)
+            sub("11", 0, (0, 2), (0, 2), 0)
+            weigh("10", (0, 4), (2, 3), k=6)
+            unload_t("11", 2, 2)
+            mx(3, 3, "G1", "d1", 0, stop=True)
+            turn_box("11", 1, (2, 4), (0, 2))
+            weigh("11", (0, 2), (0, 2))
+            unload_t("11", 3, 3)
+            sub("11", 1, (2, 3), (0, 2), 0)
+            turn_col("11", 2, 2)
+            sub("11", 2, (0, 3), (2, 3), 0)
+            store("01", (0, 2), (0, 4))
+            store("00", (2, 4), (0, 4))
+            store("10", (0, 4), (0, 2))
+            turn_col("11", 3, 3)
+            sub("11", 2, (3, 4), (2, 3), 3)
+            sub("11", 3, (0, 4), (3, 4), 0)
+            store("11", (0, 2), (0, 2))
+            store("10", (0, 4), (2, 4))
+            sub("11", 1, (3, 4), (0, 2), 2)
+            weigh("11", (0, 4), (3, 4))
+            weigh("11", (3, 4), (0, 3))
+            store("11", (0, 4), (3, 4))
+            weigh("11", (2, 3), (0, 2))
+            store("11", (2, 4), (0, 2))
+            weigh("11", (0, 3), (2, 3))
+            store("11", (0, 4), (2, 3))

@@ -66,7 +66,7 @@ def tile_commutator_directional_derivative_e4_kernel(tc, g_words, g_scales, d, f
         def load_g_scales():
             nc.vector.memset(g_plane[:].rearrange("p g n -> p (g n)").bitcast(I32), 0)
             for q in range(4):
-                nc.scalar.dma_start(out=g_plane[32 * q:32 * q + 4, :, :].bitcast(I32), in_=g_scales[:, 4 * q:4 * q + 4, :].rearrange("g r n -> r g n").bitcast(I32))
+                nc.gpsimd.dma_start(out=g_plane[32 * q:32 * q + 4, :, :].bitcast(I32), in_=g_scales[:, 4 * q:4 * q + 4, :].rearrange("g r n -> r g n").bitcast(I32))
             nc.vector.memset(warm[:, 0:1], 0.0)
             nc.scalar.mul(out=warm[:, 1:2], in_=warm[:, 0:1], mul=-1.0)
 
@@ -117,11 +117,12 @@ def tile_commutator_directional_derivative_e4_kernel(tc, g_words, g_scales, d, f
             for a in range(TILES):
                 mx(k0 + a, a, stat, mov, g, start, stop)
 
-        def unload_t(q, k, a):
+        def unload_t(q, k, a, b0=0, b1=TILES):
+            cols = slice(b0 * P, b1 * P)
             if q == "01":
-                nc.scalar.mul(out=t_sb[q][:, a, :], in_=bank[k][:], mul=-1.0)
+                nc.scalar.mul(out=t_sb[q][:, a, cols], in_=bank[k][:, cols], mul=-1.0)
             else:
-                nc.scalar.copy(out=t_sb[q][:, a, :], in_=bank[k][:])
+                nc.scalar.copy(out=t_sb[q][:, a, cols], in_=bank[k][:, cols])
 
         def turn(k, slot, q, a, b):
             nc.tensor.transpose(bank[k][:, slot * P:(slot + 1) * P], t_sb[q][:, a, b * P:(b + 1) * P], ident[:])
@@ -167,202 +168,207 @@ def tile_commutator_directional_derivative_e4_kernel(tc, g_words, g_scales, d, f
             make_identity(nc, ident[:])
             load_f(1)
             load_g_scales()
-            turn_f(1, 5)
-            load_x("d", 0, 1)
-            group("S", "d", 0, 1, 128, 256)
-            load_x("d", 0, 0, 0, 256)
-            load_f(2)
-            load_g(0, 1, 2)
-            group("S", "d", 0, 1, 448, 512)
-            turn_f(2, 6)
-            group("V", "d", 0, 1, 0, 128)
-            quant("d", 0, 1, 0, 256)
-            turn_f(3, 7)
             load_f(0)
-            load_x("r", 0, 0)
-            group("V", "d", 0, 1, 256, 448)
-            group("V", "d", 0, 0, 0, 128)
-            quant("d", 0, 1, 256, 512)
-            turn_f(0, 4)
-            mx(2, 2, "d0", "G0", 1, start=True)
-            mx(3, 3, "d0", "G0", 1, start=True)
-            load_f(6)
+            load_f(2)
+            load_x("r", 0, 0, 0, 256)
             load_f(4)
-            group("S", "d", 0, 0, 128, 256)
-            unload_f(2, 6)
-            load_x("r", 0, 1)
-            unload_f(3, 7)
-            unload_f(1, 5)
-            quant("f", 0, 1, 256, 512)
-            group("V", "r", 0, 0, 256, 512)
-            quant("f", 0, 0, 256, 512)
-            mx(1, 1, "d0", "G0", 1, start=True)
-            quant("r", 0, 0, 256, 512)
-            unload_f(0, 4)
-            group("V", "r", 0, 0, 0, 256)
-            turn_f(7, 7)
-            quant("f", 0, 0, 0, 256)
-            quant("f", 0, 1, 0, 256)
-            turn_f(6, 6)
-            quant("r", 0, 0, 0, 256)
-            group("V", "r", 0, 1, 0, 256)
-            quant("d", 0, 0, 0, 256)
-            unload_f(7, 7)
-            unload_f(6, 6)
-            turn_f(5, 5)
-            turn_f(4, 4)
-            mx(2, 2, "r0", "f0", 0)
-            quant("f", 1, 1, 256, 512)
-            unload_f(5, 5)
-            unload_f(4, 4)
-            quant("f", 1, 1, 0, 256)
-            load_g(1, 0, 2)
-            load_g(0, 0, 1)
             load_x("d", 0, 0, 256, 512)
-            load_x("r", 1, 0)
-            mx(3, 3, "r0", "f0", 0)
+            load_x("r", 0, 1, 0, 256)
+            turn_f(1, 5)
+            load_f(6)
+            group("V", "r", 0, 0, 0, 224)
+            unload_f(1, 5)
+            load_x("d", 0, 0, 0, 256)
+            load_x("r", 0, 1, 256, 512)
+            load_g(0, 0, 1)
+            load_g(1, 0, 2)
+            turn_f(0, 4)
+            turn_f(2, 6)
+            unload_f(0, 4)
+            quant("f", 0, 1, 0, 256)
+            turn_f(3, 7)
+            group("S", "r", 0, 0, 224, 256)
+            unload_f(2, 6)
+            unload_f(3, 7)
+            turn_f(5, 5)
+            group("S", "d", 0, 0, 256, 512)
+            unload_f(5, 5)
+            quant("r", 0, 0, 0, 256)
+            turn_f(4, 4)
+            quant("f", 0, 0, 0, 256)
+            quant("f", 0, 0, 256, 512)
+            group("V", "r", 0, 1, 0, 256)
             mx(0, 0, "r0", "f0", 0, start=True)
-            mx(1, 1, "r0", "f0", 0)
-            load_x("d", 1, 0)
-            group("S", "r", 0, 1, 256, 512)
-            load_x("d", 1, 1)
-            group("S", "d", 0, 0, 352, 512)
-            group("S", "r", 1, 0, 160, 512)
-            group("S", "d", 1, 0, 448, 512)
-            mx(0, 0, "d0", "G0", 1)
-            quant("r", 0, 1, 0, 256)
-            mx(7, 3, "d0", "G1", 1, start=True)
-            mx(5, 1, "d0", "G1", 0, start=True)
-            mx(4, 0, "d0", "G1", 1, start=True)
-            group("V", "d", 0, 0, 256, 352)
-            mx(5, 1, "d0", "G1", 1)
+            load_x("r", 0, 0, 256, 512)
+            load_x("d", 0, 1, 0, 256)
+            load_x("d", 0, 1, 256, 512)
+            unload_f(4, 4)
+            mx(1, 1, "r0", "f0", 0, start=True)
             load_x("r", 1, 1)
-            mx(0, 0, "d0", "G0", 0)
-            mx(5, 1, "r0", "f1", 1)
-            load_w(1)
-            load_w(0)
-            quant("f", 1, 0, 0, 256)
-            mx(1, 1, "d0", "G0", 0)
-            mx(4, 0, "d0", "G1", 0)
-            quant("f", 1, 0, 256, 512)
+            group("S", "r", 0, 1, 352, 512)
+            quant("f", 0, 1, 256, 512)
+            quant("r", 0, 1, 0, 256)
+            turn_f(6, 6)
+            turn_f(7, 7)
+            mx(0, 0, "r0", "f0", 1)
+            unload_f(6, 6)
+            unload_f(7, 7)
+            group("S", "r", 0, 0, 256, 512)
+            load_g(0, 1, 2)
+            load_x("r", 1, 0)
+            load_x("d", 1, 0)
+            load_x("d", 1, 1)
             quant("d", 0, 0, 256, 512)
-            mx(4, 0, "r0", "f1", 1)
-            mx(4, 0, "r0", "f1", 0)
-            mx(0, 0, "r0", "f0", 1, stop=True)
-            mx(6, 2, "d0", "G1", 0, start=True)
-            mx(1, 1, "r0", "f0", 1, stop=True)
-            unload_t("00", 1, 1)
-            group("V", "r", 1, 0, 0, 160)
+            group("S", "d", 0, 1, 256, 512)
+            group("V", "d", 0, 0, 0, 256)
+            load_w(0)
+            group("V", "r", 0, 1, 256, 352)
+            mx(1, 1, "r0", "f0", 1)
+            quant("d", 0, 0, 0, 256)
+            mx(3, 3, "d0", "G0", 0, start=True)
+            mx(2, 2, "d0", "G0", 0, start=True)
+            mx(0, 0, "d0", "G0", 0)
             quant("r", 0, 1, 256, 512)
-            group("V", "d", 1, 0, 0, 448)
-            quant("r", 1, 0, 0, 512)
-            unload_t("00", 0, 0)
-            mx(2, 2, "d0", "G0", 0)
-            mx(7, 3, "d0", "G1", 0)
-            mx(5, 1, "r0", "f1", 0)
+            quant("f", 1, 0, 0, 256)
+            group("S", "r", 1, 1, 352, 512)
+            mx(1, 1, "d0", "G0", 0)
+            quant("f", 1, 1, 0, 256)
+            quant("f", 1, 1, 256, 512)
+            mx(2, 2, "r0", "f0", 1)
+            mx(5, 1, "d0", "G1", 0, start=True)
+            mx(7, 3, "d0", "G1", 0, start=True)
+            mx(6, 2, "d0", "G1", 0, start=True)
             mx(3, 3, "r0", "f0", 1)
-            mx(2, 2, "r0", "f0", 1, stop=True)
-            mx(7, 3, "r0", "f1", 0)
+            quant("f", 1, 0, 256, 512)
+            mx(7, 3, "r0", "f1", 1)
+            mx(4, 0, "r0", "f1", 0, start=True)
+            mx(4, 0, "r0", "f1", 1)
+            group("V", "d", 0, 1, 0, 256)
+            mx(5, 1, "r0", "f1", 1)
+            mx(4, 0, "d0", "G1", 0)
+            quant("r", 0, 0, 256, 512)
+            quant("d", 0, 1, 0, 256)
             mx(6, 2, "r0", "f1", 1)
-            mx(3, 3, "d0", "G0", 0, stop=True)
+            mx(5, 1, "r0", "f1", 0)
+            mx(3, 3, "r0", "f0", 0)
+            mx(7, 3, "r0", "f1", 0)
+            mx(2, 2, "r0", "f0", 0)
+            group("V", "r", 1, 1, 0, 352)
+            quant("d", 0, 1, 256, 512)
+            quant("r", 1, 1, 0, 512)
+            group("V", "r", 1, 0, 0, 512)
+            group("V", "d", 1, 0, 0, 352)
+            mx(0, 0, "d0", "G0", 1, stop=True)
+            unload_t("00", 0, 0)
+            mx(1, 1, "d0", "G0", 1, stop=True)
+            mx(5, 1, "d0", "G1", 1)
+            mx(4, 0, "d0", "G1", 1)
+            mx(2, 2, "d0", "G0", 1, stop=True)
+            mx(3, 3, "d0", "G0", 1, stop=True)
+            mx(7, 3, "f0", "r1", 1)
+            mx(6, 2, "d0", "G1", 1)
+            mx(6, 2, "f0", "r1", 1)
+            mx(6, 2, "r0", "f1", 0)
+            unload_t("00", 1, 1)
+            unload_t("00", 2, 2)
+            mx(5, 1, "f0", "r1", 1)
+            mx(4, 0, "f0", "r1", 1)
+            mx(7, 3, "d0", "G1", 1)
+            unload_t("00", 3, 3)
+            turn_row("00", 1, 1, 4)
+            turn_row("00", 0, 0, 4)
+            group("S", "d", 1, 0, 352, 512)
+            quant("r", 1, 0, 0, 512)
             quant("d", 1, 0, 0, 512)
             group("V", "d", 1, 1, 0, 160)
-            unload_t("00", 2, 2)
-            unload_t("00", 3, 3)
-            mx(6, 2, "d0", "G1", 1)
-            mx(6, 2, "f0", "r1", 0)
-            mx(4, 0, "G0", "d1", 0)
-            mx(7, 3, "f0", "r1", 0)
-            group("V", "r", 1, 1, 0, 384)
-            mx(7, 3, "G0", "d1", 0)
-            turn_row("00", 0, 0, 4)
-            turn_row("00", 1, 1, 4)
-            turn_row("00", 3, 3, 4)
             turn_row("00", 2, 2, 4)
-            mx(4, 0, "f0", "r1", 0)
-            mx(6, 2, "r0", "f1", 0)
-            mx(6, 2, "G0", "d1", 0)
-            group("S", "r", 1, 1, 384, 512)
             group("S", "d", 1, 1, 160, 512)
-            quant("r", 1, 1, 0, 512)
-            sub("00", 1, (1, 2), (0, 4))
-            sub("00", 3, (3, 4), (0, 4))
-            quant("d", 1, 1, 0, 512)
-            mx(1, 1, "f1", "r1", 1, start=True)
-            mx(4, 0, "f0", "r1", 1)
-            mx(5, 1, "G0", "d1", 0)
-            mx(7, 3, "r0", "f1", 1)
+            turn_row("00", 3, 3, 4)
+            mx(7, 3, "f0", "r1", 0)
             sub("00", 0, (0, 1), (0, 4))
-            weigh("00", (3, 4), (0, 4))
-            weigh("00", (1, 2), (0, 4))
-            sub("00", 2, (2, 3), (0, 4))
-            mx(7, 3, "f0", "r1", 1)
-            mx(7, 3, "G0", "d1", 1, stop=True)
+            mx(5, 1, "f0", "r1", 0)
+            mx(7, 3, "G0", "d1", 0)
+            mx(6, 2, "f0", "r1", 0)
+            mx(4, 0, "f0", "r1", 0)
+            mx(4, 0, "G0", "d1", 0)
+            mx(6, 2, "G0", "d1", 0)
+            mx(5, 1, "G0", "d1", 0)
+            mx(0, 0, "f1", "r1", 0, start=True)
+            quant("d", 1, 1, 0, 512)
             mx(4, 0, "G0", "d1", 1, stop=True)
-            weigh("00", (0, 1), (0, 4))
-            mx(6, 2, "f0", "r1", 1)
-            mx(5, 1, "G0", "d1", 1)
-            unload_t("01", 4, 0)
+            sub("00", 1, (1, 2), (0, 4))
+            mx(5, 1, "G0", "d1", 1, stop=True)
+            mx(1, 1, "G1", "d1", 1, start=True)
+            mx(1, 1, "f1", "r1", 0)
+            mx(7, 3, "G0", "d1", 1, stop=True)
+            load_w(1)
             mx(6, 2, "G0", "d1", 1, stop=True)
-            mx(0, 0, "G1", "d1", 0, start=True)
-            unload_t("01", 7, 3)
-            mx(5, 1, "f0", "r1", 1)
-            mx(5, 1, "f0", "r1", 0, stop=True)
-            mx(0, 0, "f1", "r1", 1)
-            mx(1, 1, "G1", "d1", 0)
+            mx(0, 0, "G1", "d1", 1)
+            sub("00", 3, (3, 4), (0, 4))
+            mx(1, 1, "f1", "r1", 1)
+            mx(1, 1, "G1", "d1", 0, stop=True)
+            mx(0, 0, "G1", "d1", 0)
+            weigh("00", (0, 1), (0, 4), eng=nc.gpsimd)
+            sub("00", 2, (2, 3), (0, 4))
+            mx(0, 0, "f1", "r1", 1, stop=True)
+            mx(2, 2, "f1", "r1", 1, start=True)
+            mx(2, 2, "G1", "d1", 0)
+            unload_t("01", 4, 0)
             weigh("01", (0, 1), (0, 4), k=4)
-            store("00", (0, 2), (0, 4))
-            mx(0, 0, "f1", "r1", 0)
+            weigh("00", (1, 2), (0, 4), eng=nc.gpsimd)
+            weigh("00", (2, 3), (0, 4), eng=nc.gpsimd)
+            weigh("00", (3, 4), (0, 4), eng=nc.gpsimd)
+            mx(2, 2, "G1", "d1", 1)
             unload_t("01", 5, 1)
+            mx(2, 2, "f1", "r1", 0, stop=True)
+            weigh("01", (1, 2), (0, 4), k=5)
+            unload_t("01", 7, 3)
+            store("00", (0, 2), (0, 4))
             unload_t("01", 6, 2)
-            mx(0, 0, "G1", "d1", 1, stop=True)
-            mx(2, 2, "G1", "d1", 0, start=True)
-            mx(1, 1, "G1", "d1", 1)
-            unload_t("11", 0, 0)
-            mx(1, 1, "f1", "r1", 0, stop=True)
             unload_t("11", 1, 1)
             weigh("01", (3, 4), (0, 4), k=7)
-            turn_col("01", 7, 3)
-            turn_col("01", 4, 0)
-            weigh("01", (1, 2), (0, 4), k=5)
             weigh("01", (2, 3), (0, 4), k=6)
-            weigh("00", (2, 3), (0, 4))
+            unload_t("11", 0, 0)
+            turn_col("01", 4, 0)
             weigh("10", (0, 4), (0, 1), k=4)
             turn_col("01", 5, 1)
-            weigh("10", (0, 4), (1, 2), k=5)
-            turn_col("01", 6, 2)
             turn_box("11", 0, (0, 2), (0, 2))
-            mx(2, 2, "G1", "d1", 1)
-            mx(2, 2, "f1", "r1", 1)
-            store("01", (2, 4), (0, 4))
-            mx(2, 2, "f1", "r1", 0, stop=True)
-            mx(3, 3, "f1", "r1", 1, start=True)
-            mx(3, 3, "G1", "d1", 1)
-            mx(3, 3, "f1", "r1", 0)
-            weigh("10", (0, 4), (3, 4), k=7)
-            sub("11", 0, (0, 2), (0, 2), 0)
-            weigh("10", (0, 4), (2, 3), k=6)
+            turn_col("01", 6, 2)
             unload_t("11", 2, 2)
-            mx(3, 3, "G1", "d1", 0, stop=True)
-            turn_box("11", 1, (2, 4), (0, 2))
-            weigh("11", (0, 2), (0, 2))
-            unload_t("11", 3, 3)
-            sub("11", 1, (2, 3), (0, 2), 0)
             turn_col("11", 2, 2)
+            mx(3, 3, "G1", "d1", 1, start=True)
+            mx(3, 3, "f1", "r1", 0)
+            mx(3, 3, "f1", "r1", 1)
+            mx(3, 3, "G1", "d1", 0, stop=True)
+            unload_t("11", 3, 3, 0, 2)
+            sub("11", 0, (0, 2), (0, 2), 0)
+            weigh("11", (0, 2), (0, 2), eng=nc.gpsimd)
+            unload_t("11", 3, 3, 2, 4)
+            turn_col("01", 7, 3)
+            weigh("10", (0, 4), (1, 2), k=5)
             sub("11", 2, (0, 3), (2, 3), 0)
             store("01", (0, 2), (0, 4))
+            weigh("10", (0, 4), (2, 3), k=6)
+            turn_box("11", 1, (2, 4), (0, 2))
+            weigh("10", (0, 4), (3, 4), k=7)
+            turn_box("11", 0, (0, 2), (3, 4))
+            sub("11", 1, (3, 4), (0, 2), 2)
+            store("01", (2, 4), (0, 4))
             store("00", (2, 4), (0, 4))
             store("10", (0, 4), (0, 2))
-            turn_col("11", 3, 3)
             sub("11", 2, (3, 4), (2, 3), 3)
-            sub("11", 3, (0, 4), (3, 4), 0)
-            store("11", (0, 2), (0, 2))
-            store("10", (0, 4), (2, 4))
-            sub("11", 1, (3, 4), (0, 2), 2)
-            weigh("11", (0, 4), (3, 4))
+            turn_box("11", 3, (2, 4), (3, 4))
+            sub("11", 1, (2, 3), (0, 2), 0)
             weigh("11", (3, 4), (0, 3))
-            store("11", (0, 4), (3, 4))
-            weigh("11", (2, 3), (0, 2))
-            store("11", (2, 4), (0, 2))
-            weigh("11", (0, 3), (2, 3))
+            weigh("11", (0, 3), (2, 3), eng=nc.gpsimd)
+            sub("11", 3, (2, 4), (3, 4), 0)
+            sub("11", 0, (0, 2), (3, 4), 0)
+            weigh("11", (2, 4), (3, 4))
+            store("11", (0, 2), (0, 2))
+            weigh("11", (2, 3), (0, 2), eng=nc.gpsimd)
+            store("10", (0, 4), (2, 4))
+            weigh("11", (0, 2), (3, 4))
             store("11", (0, 4), (2, 3))
+            store("11", (2, 4), (0, 2))
+            store("11", (2, 4), (3, 4))
+            store("11", (0, 2), (3, 4))

@@ -37,7 +37,7 @@ def tile_commutator_directional_derivative_e4_kernel(tc, g_words, g_scales, d, f
         f_grouped = [sb.tile([P, 2, H, PACK], BF16, name="grp_f%d" % h, align_bytes=64) for h in range(2)]
         codes = {(x, h, g): sb.tile([P, H], U32, name="codes_%s%d%d" % (x, h, g), align_bytes=64) for x in "drf" for h, g in pieces}
         scales = {(x, h, g): sb.tile([P, H], U8, name="scales_%s%d%d" % (x, h, g), align_bytes=64) for x in "drf" for h, g in pieces}
-        g_codes = [sb.tile([P, 2, H], U32, name="g_codes%d" % h, align_bytes=64) for h in range(2)]
+        g_codes = [sb.tile([P, N], U32, name="g_codes%d" % g, align_bytes=64) for g in range(2)]
         warm = sb.tile([P, 8], F32, name="warm")
         g_plane = sb.tile([P, 2, N], U8, name="g_plane", align_bytes=64)
         f_raw = [sb.tile([P, N], BF16, name="f_raw%d" % m) for m in range(2)]
@@ -59,9 +59,8 @@ def tile_commutator_directional_derivative_e4_kernel(tc, g_words, g_scales, d, f
         def load_x(x, h, g, c0=0, c1=H):
             nc.sync.dma_start(out=raw[x, h, g][:, :, c0:c1], in_=src[x][g * KP:(g + 1) * KP, h * H + c0:h * H + c1].rearrange("(p t) c -> p t c", t=PACK))
 
-        def load_g(h, g0, g1):
-            words = g_words[g0:g1].rearrange("g p n t -> p g (n t)")[:, :, h * H * PACK:(h + 1) * H * PACK]
-            nc.sync.dma_start(out=g_codes[h][:, g0:g1, :].bitcast(I32), in_=words.bitcast(I32))
+        def load_g(g):
+            nc.sync.dma_start(out=g_codes[g][:].bitcast(I32), in_=g_words[g].rearrange("p n t -> p (n t)").bitcast(I32))
 
         def load_g_scales():
             nc.vector.memset(g_plane[:].rearrange("p g n -> p (g n)").bitcast(I32), 0)
@@ -105,7 +104,7 @@ def tile_commutator_directional_derivative_e4_kernel(tc, g_words, g_scales, d, f
 
         def operand(x, h, g, c0, c1):
             if x == "G":
-                return g_codes[h][:, g, c0:c1].bitcast(E5M2), g_plane[:, g, h * H + c0:h * H + c1]
+                return g_codes[g][:, h * H + c0:h * H + c1].bitcast(E5M2), g_plane[:, g, h * H + c0:h * H + c1]
             return codes[x, h, g][:, c0:c1].bitcast(E4M3), scales[x, h, g][:, c0:c1]
 
         def mx(k, a, stat, mov, g, start=False, stop=False):
@@ -166,209 +165,202 @@ def tile_commutator_directional_derivative_e4_kernel(tc, g_words, g_scales, d, f
 
         with tc.manual_schedule():
             make_identity(nc, ident[:])
-            load_f(1)
-            load_g_scales()
             load_f(0)
+            load_g_scales()
+            load_f(1)
             load_f(2)
-            load_x("r", 0, 0, 0, 256)
+            load_x("r", 0, 0)
             load_f(4)
-            load_x("d", 0, 0, 256, 512)
-            load_x("r", 0, 1, 0, 256)
-            turn_f(1, 5)
             load_f(6)
-            group("V", "r", 0, 0, 0, 224)
-            unload_f(1, 5)
-            load_x("d", 0, 0, 0, 256)
-            load_x("r", 0, 1, 256, 512)
-            load_g(0, 0, 1)
-            load_g(1, 0, 2)
+            load_x("d", 0, 0)
+            load_g(0)
             turn_f(0, 4)
+            turn_f(1, 5)
             turn_f(2, 6)
-            unload_f(0, 4)
-            quant("f", 0, 1, 0, 256)
             turn_f(3, 7)
-            group("S", "r", 0, 0, 224, 256)
-            unload_f(2, 6)
-            unload_f(3, 7)
-            turn_f(5, 5)
-            group("S", "d", 0, 0, 256, 512)
-            unload_f(5, 5)
-            quant("r", 0, 0, 0, 256)
-            turn_f(4, 4)
-            quant("f", 0, 0, 0, 256)
-            quant("f", 0, 0, 256, 512)
-            group("V", "r", 0, 1, 0, 256)
-            mx(0, 0, "r0", "f0", 0, start=True)
-            load_x("r", 0, 0, 256, 512)
-            load_x("d", 0, 1, 0, 256)
-            load_x("d", 0, 1, 256, 512)
-            unload_f(4, 4)
-            mx(1, 1, "r0", "f0", 0, start=True)
-            load_x("r", 1, 1)
-            group("S", "r", 0, 1, 352, 512)
-            quant("f", 0, 1, 256, 512)
-            quant("r", 0, 1, 0, 256)
-            turn_f(6, 6)
-            turn_f(7, 7)
-            mx(0, 0, "r0", "f0", 1)
-            unload_f(6, 6)
-            unload_f(7, 7)
-            group("S", "r", 0, 0, 256, 512)
-            load_g(0, 1, 2)
+            unload_f(0, 4)
+            load_x("r", 0, 1)
+            load_x("d", 0, 1)
+            unload_f(1, 5)
+            quant("f", 0, 1, 0, 256)
             load_x("r", 1, 0)
+            group("V", "r", 0, 0, 0, 256)
+            quant("f", 0, 0, 0, 256)
+            quant("r", 0, 0, 0, 256)
+            unload_f(2, 6)
+            turn_f(4, 4)
+            load_g(1)
             load_x("d", 1, 0)
             load_x("d", 1, 1)
-            quant("d", 0, 0, 256, 512)
-            group("S", "d", 0, 1, 256, 512)
-            group("V", "d", 0, 0, 0, 256)
+            load_x("r", 1, 1)
+            turn_f(5, 5)
+            unload_f(3, 7)
+            quant("f", 0, 0, 256, 512)
+            mx(0, 0, "r0", "f0", 0, start=True)
+            mx(1, 1, "r0", "f0", 0, start=True)
+            unload_f(4, 4)
+            unload_f(5, 5)
+            group("S", "d", 0, 0, 160, 256)
+            group("V", "r", 0, 0, 256, 512)
+            quant("f", 0, 1, 256, 512)
+            quant("r", 0, 0, 256, 512)
+            turn_f(6, 6)
+            group("S", "d", 0, 0, 384, 512)
+            unload_f(6, 6)
+            group("V", "d", 0, 0, 0, 160)
             load_w(0)
-            group("V", "r", 0, 1, 256, 352)
-            mx(1, 1, "r0", "f0", 1)
+            turn_f(7, 7)
+            mx(2, 2, "r0", "f0", 0, start=True)
+            mx(3, 3, "r0", "f0", 0, start=True)
             quant("d", 0, 0, 0, 256)
-            mx(3, 3, "d0", "G0", 0, start=True)
-            mx(2, 2, "d0", "G0", 0, start=True)
-            mx(0, 0, "d0", "G0", 0)
-            quant("r", 0, 1, 256, 512)
+            unload_f(7, 7)
+            group("V", "d", 0, 0, 256, 384)
             quant("f", 1, 0, 0, 256)
-            group("S", "r", 1, 1, 352, 512)
-            mx(1, 1, "d0", "G0", 0)
+            quant("d", 0, 0, 256, 512)
             quant("f", 1, 1, 0, 256)
             quant("f", 1, 1, 256, 512)
-            mx(2, 2, "r0", "f0", 1)
-            mx(5, 1, "d0", "G1", 0, start=True)
-            mx(7, 3, "d0", "G1", 0, start=True)
-            mx(6, 2, "d0", "G1", 0, start=True)
-            mx(3, 3, "r0", "f0", 1)
             quant("f", 1, 0, 256, 512)
-            mx(7, 3, "r0", "f1", 1)
-            mx(4, 0, "r0", "f1", 0, start=True)
-            mx(4, 0, "r0", "f1", 1)
-            group("V", "d", 0, 1, 0, 256)
-            mx(5, 1, "r0", "f1", 1)
-            mx(4, 0, "d0", "G1", 0)
-            quant("r", 0, 0, 256, 512)
-            quant("d", 0, 1, 0, 256)
-            mx(6, 2, "r0", "f1", 1)
+            mx(0, 0, "d0", "G0", 0)
+            mx(1, 1, "d0", "G0", 0)
+            mx(4, 0, "d0", "G1", 0, start=True)
+            mx(5, 1, "d0", "G1", 0, start=True)
+            mx(2, 2, "d0", "G0", 0)
+            mx(3, 3, "d0", "G0", 0)
+            group("V", "r", 0, 1, 256, 512)
+            group("S", "r", 0, 1, 0, 256)
+            group("S", "d", 0, 1, 0, 256)
+            quant("r", 0, 1, 0, 256)
+            quant("r", 0, 1, 256, 512)
+            mx(6, 2, "d0", "G1", 0, start=True)
+            mx(7, 3, "d0", "G1", 0, start=True)
+            group("S", "r", 1, 0, 192, 512)
+            mx(4, 0, "r0", "f1", 0)
             mx(5, 1, "r0", "f1", 0)
-            mx(3, 3, "r0", "f0", 0)
+            mx(6, 2, "r0", "f1", 0)
             mx(7, 3, "r0", "f1", 0)
-            mx(2, 2, "r0", "f0", 0)
-            group("V", "r", 1, 1, 0, 352)
+            mx(4, 0, "r0", "f1", 1)
+            mx(5, 1, "r0", "f1", 1)
+            group("V", "d", 0, 1, 256, 512)
+            quant("d", 0, 1, 0, 256)
             quant("d", 0, 1, 256, 512)
-            quant("r", 1, 1, 0, 512)
-            group("V", "r", 1, 0, 0, 512)
-            group("V", "d", 1, 0, 0, 352)
+            group("V", "r", 1, 0, 0, 192)
+            quant("r", 1, 0, 0, 512)
+            group("V", "d", 1, 0, 0, 512)
+            group("V", "d", 1, 1, 0, 512)
+            mx(0, 0, "r0", "f0", 1)
+            mx(1, 1, "r0", "f0", 1)
+            mx(2, 2, "r0", "f0", 1)
+            mx(3, 3, "r0", "f0", 1)
             mx(0, 0, "d0", "G0", 1, stop=True)
-            unload_t("00", 0, 0)
             mx(1, 1, "d0", "G0", 1, stop=True)
-            mx(5, 1, "d0", "G1", 1)
-            mx(4, 0, "d0", "G1", 1)
             mx(2, 2, "d0", "G0", 1, stop=True)
             mx(3, 3, "d0", "G0", 1, stop=True)
-            mx(7, 3, "f0", "r1", 1)
-            mx(6, 2, "d0", "G1", 1)
-            mx(6, 2, "f0", "r1", 1)
-            mx(6, 2, "r0", "f1", 0)
-            unload_t("00", 1, 1)
-            unload_t("00", 2, 2)
-            mx(5, 1, "f0", "r1", 1)
-            mx(4, 0, "f0", "r1", 1)
-            mx(7, 3, "d0", "G1", 1)
-            unload_t("00", 3, 3)
-            turn_row("00", 1, 1, 4)
-            turn_row("00", 0, 0, 4)
-            group("S", "d", 1, 0, 352, 512)
-            quant("r", 1, 0, 0, 512)
             quant("d", 1, 0, 0, 512)
-            group("V", "d", 1, 1, 0, 160)
-            turn_row("00", 2, 2, 4)
-            group("S", "d", 1, 1, 160, 512)
-            turn_row("00", 3, 3, 4)
-            mx(7, 3, "f0", "r1", 0)
-            sub("00", 0, (0, 1), (0, 4))
-            mx(5, 1, "f0", "r1", 0)
-            mx(7, 3, "G0", "d1", 0)
-            mx(6, 2, "f0", "r1", 0)
+            unload_t("00", 0, 0)
+            unload_t("00", 1, 1)
+            mx(4, 0, "d0", "G1", 1)
+            mx(5, 1, "d0", "G1", 1)
+            mx(6, 2, "r0", "f1", 1)
+            mx(7, 3, "r0", "f1", 1)
+            mx(6, 2, "d0", "G1", 1)
+            mx(7, 3, "d0", "G1", 1)
+            unload_t("00", 2, 2)
+            unload_t("00", 3, 3)
+            group("S", "r", 1, 1, 128, 512)
             mx(4, 0, "f0", "r1", 0)
+            mx(5, 1, "f0", "r1", 0)
+            mx(6, 2, "f0", "r1", 0)
+            mx(7, 3, "f0", "r1", 0)
+            turn_row("00", 0, 0, 4)
+            turn_row("00", 1, 1, 4)
+            turn_row("00", 2, 2, 4)
+            turn_row("00", 3, 3, 4)
             mx(4, 0, "G0", "d1", 0)
-            mx(6, 2, "G0", "d1", 0)
             mx(5, 1, "G0", "d1", 0)
-            mx(0, 0, "f1", "r1", 0, start=True)
+            mx(6, 2, "G0", "d1", 0)
+            mx(7, 3, "G0", "d1", 0)
+            group("V", "r", 1, 1, 0, 128)
             quant("d", 1, 1, 0, 512)
-            mx(4, 0, "G0", "d1", 1, stop=True)
+            sub("00", 0, (0, 1), (0, 4))
+            quant("r", 1, 1, 0, 512)
             sub("00", 1, (1, 2), (0, 4))
-            mx(5, 1, "G0", "d1", 1, stop=True)
-            mx(1, 1, "G1", "d1", 1, start=True)
-            mx(1, 1, "f1", "r1", 0)
-            mx(7, 3, "G0", "d1", 1, stop=True)
-            load_w(1)
-            mx(6, 2, "G0", "d1", 1, stop=True)
-            mx(0, 0, "G1", "d1", 1)
-            sub("00", 3, (3, 4), (0, 4))
-            mx(1, 1, "f1", "r1", 1)
-            mx(1, 1, "G1", "d1", 0, stop=True)
-            mx(0, 0, "G1", "d1", 0)
-            weigh("00", (0, 1), (0, 4), eng=nc.gpsimd)
             sub("00", 2, (2, 3), (0, 4))
-            mx(0, 0, "f1", "r1", 1, stop=True)
-            mx(2, 2, "f1", "r1", 1, start=True)
-            mx(2, 2, "G1", "d1", 0)
+            mx(4, 0, "G0", "d1", 1)
+            mx(5, 1, "G0", "d1", 1)
+            mx(6, 2, "G0", "d1", 1)
+            mx(7, 3, "G0", "d1", 1)
+            weigh("00", (0, 1), (0, 4), eng=nc.gpsimd)
+            mx(4, 0, "f0", "r1", 1, stop=True)
+            mx(5, 1, "f0", "r1", 1, stop=True)
+            mx(6, 2, "f0", "r1", 1, stop=True)
+            mx(7, 3, "f0", "r1", 1, stop=True)
             unload_t("01", 4, 0)
-            weigh("01", (0, 1), (0, 4), k=4)
-            weigh("00", (1, 2), (0, 4), eng=nc.gpsimd)
-            weigh("00", (2, 3), (0, 4), eng=nc.gpsimd)
-            weigh("00", (3, 4), (0, 4), eng=nc.gpsimd)
-            mx(2, 2, "G1", "d1", 1)
             unload_t("01", 5, 1)
-            mx(2, 2, "f1", "r1", 0, stop=True)
+            mx(0, 0, "G1", "d1", 0, start=True)
+            mx(0, 0, "G1", "d1", 1)
+            mx(1, 1, "G1", "d1", 0, start=True)
+            mx(1, 1, "G1", "d1", 1)
+            sub("00", 3, (3, 4), (0, 4))
+            weigh("01", (0, 1), (0, 4), k=4)
             weigh("01", (1, 2), (0, 4), k=5)
-            unload_t("01", 7, 3)
-            store("00", (0, 2), (0, 4))
             unload_t("01", 6, 2)
-            unload_t("11", 1, 1)
-            weigh("01", (3, 4), (0, 4), k=7)
-            weigh("01", (2, 3), (0, 4), k=6)
+            mx(0, 0, "f1", "r1", 0)
+            mx(0, 0, "f1", "r1", 1, stop=True)
+            mx(1, 1, "f1", "r1", 0)
+            mx(1, 1, "f1", "r1", 1, stop=True)
+            unload_t("01", 7, 3)
             unload_t("11", 0, 0)
-            turn_col("01", 4, 0)
-            weigh("10", (0, 4), (0, 1), k=4)
-            turn_col("01", 5, 1)
+            unload_t("11", 1, 1)
+            mx(2, 2, "G1", "d1", 0, start=True)
+            mx(2, 2, "G1", "d1", 1)
+            turn_row("01", 4, 0, 4)
+            weigh("00", (1, 2), (0, 4), eng=nc.gpsimd)
+            mx(2, 2, "f1", "r1", 0)
+            mx(2, 2, "f1", "r1", 1, stop=True)
+            load_w(1)
+            weigh("00", (2, 3), (0, 4), eng=nc.gpsimd)
             turn_box("11", 0, (0, 2), (0, 2))
-            turn_col("01", 6, 2)
+            store("00", (0, 2), (0, 4))
+            weigh("01", (2, 3), (0, 4), k=6)
+            weigh("01", (3, 4), (0, 4), k=7)
+            turn_row("01", 5, 1, 4)
+            turn_row("01", 6, 2, 4)
+            turn_row("01", 7, 3, 4)
             unload_t("11", 2, 2)
             turn_col("11", 2, 2)
-            mx(3, 3, "G1", "d1", 1, start=True)
-            mx(3, 3, "f1", "r1", 0)
-            mx(3, 3, "f1", "r1", 1)
-            mx(3, 3, "G1", "d1", 0, stop=True)
-            unload_t("11", 3, 3, 0, 2)
+            weigh("10", (0, 1), (0, 4), k=4)
             sub("11", 0, (0, 2), (0, 2), 0)
+            weigh("10", (1, 2), (0, 4), k=5)
+            weigh("00", (3, 4), (0, 4), eng=nc.gpsimd)
             weigh("11", (0, 2), (0, 2), eng=nc.gpsimd)
-            unload_t("11", 3, 3, 2, 4)
-            turn_col("01", 7, 3)
-            weigh("10", (0, 4), (1, 2), k=5)
-            sub("11", 2, (0, 3), (2, 3), 0)
-            store("01", (0, 2), (0, 4))
-            weigh("10", (0, 4), (2, 3), k=6)
+            weigh("10", (2, 3), (0, 4), k=6)
+            mx(3, 3, "f1", "r1", 0, start=True)
+            mx(3, 3, "f1", "r1", 1)
+            mx(3, 3, "G1", "d1", 0)
+            mx(3, 3, "G1", "d1", 1, stop=True)
             turn_box("11", 1, (2, 4), (0, 2))
-            weigh("10", (0, 4), (3, 4), k=7)
+            unload_t("11", 3, 3, 0, 2)
+            store("01", (0, 2), (0, 4))
+            unload_t("11", 3, 3, 2, 4)
             turn_box("11", 0, (0, 2), (3, 4))
+            turn_box("11", 3, (2, 4), (3, 4))
+            sub("11", 2, (0, 3), (2, 3), 0)
+            weigh("10", (3, 4), (0, 4), k=7)
+            sub("11", 1, (2, 3), (0, 2), 0)
+            weigh("11", (0, 3), (2, 3), eng=nc.gpsimd)
+            weigh("11", (2, 3), (0, 2), eng=nc.gpsimd)
             sub("11", 1, (3, 4), (0, 2), 2)
             store("01", (2, 4), (0, 4))
             store("00", (2, 4), (0, 4))
-            store("10", (0, 4), (0, 2))
+            store("10", (0, 2), (0, 4))
+            store("10", (2, 4), (0, 4))
             sub("11", 2, (3, 4), (2, 3), 3)
-            turn_box("11", 3, (2, 4), (3, 4))
-            sub("11", 1, (2, 3), (0, 2), 0)
-            weigh("11", (3, 4), (0, 3))
-            weigh("11", (0, 3), (2, 3), eng=nc.gpsimd)
-            sub("11", 3, (2, 4), (3, 4), 0)
             sub("11", 0, (0, 2), (3, 4), 0)
-            weigh("11", (2, 4), (3, 4))
-            store("11", (0, 2), (0, 2))
-            weigh("11", (2, 3), (0, 2), eng=nc.gpsimd)
-            store("10", (0, 4), (2, 4))
+            weigh("11", (3, 4), (0, 3))
+            sub("11", 3, (2, 4), (3, 4), 0)
             weigh("11", (0, 2), (3, 4))
-            store("11", (0, 4), (2, 3))
-            store("11", (2, 4), (0, 2))
-            store("11", (2, 4), (3, 4))
+            store("11", (0, 2), (0, 3))
+            weigh("11", (2, 4), (3, 4))
+            store("11", (2, 4), (0, 3))
             store("11", (0, 2), (3, 4))
+            store("11", (2, 4), (3, 4))

@@ -18,349 +18,292 @@ SUB = mybir.AluOpType.subtract
 
 P = 128
 PACK = 4
-KP = 512
-H = 512
-TILES = 4
+GROUP = P * PACK
+HALF = N // 2
+QUARTER = N // 4
+TILES = HALF // P
+ALL = (0, TILES)
+FIRST_BANK = {"00": 0, "11": 0, "01": TILES}
+PASSES = {"00": 4, "11": 4, "01": 8}
 
 
 def tile_commutator_directional_derivative_e4_kernel(tc, g_words, g_scales, d, f, r, w, out):
     nc = tc.nc
-    src = {"d": d, "r": r}
+    vector, scalar, gpsimd = nc.vector, nc.scalar, nc.gpsimd
     with ExitStack() as ctx:
         sb = ctx.enter_context(tc.tile_pool(name="sb", bufs=1))
         ps = ctx.enter_context(tc.psum_pool(name="ps", bufs=1))
-        bank = [ps.tile([P, H], F32, name="bank%d" % k) for k in range(8)]
+        bank = [ps.tile([P, HALF], F32, name="bank%d" % k) for k in range(2 * TILES)]
+        ident_bf16 = sb.tile([P, P], BF16, name="ident_bf16")
         ident = sb.tile([P, P], F32, name="ident")
-        pieces = [(h, g) for h in range(2) for g in range(2)]
-        raw = {(x, h, g): sb.tile([P, PACK, H], BF16, name="raw_%s%d%d" % (x, h, g)) for x in "dr" for h, g in pieces}
-        grouped = {(x, h, g): sb.tile([P, H, PACK], BF16, name="grp_%s%d%d" % (x, h, g), align_bytes=64) for x in "dr" for h, g in pieces}
-        f_grouped = [sb.tile([P, 2, H, PACK], BF16, name="grp_f%d" % h, align_bytes=64) for h in range(2)]
-        codes = {(x, h, g): sb.tile([P, H], U32, name="codes_%s%d%d" % (x, h, g), align_bytes=64) for x in "drf" for h, g in pieces}
-        scales = {(x, h, g): sb.tile([P, H], U8, name="scales_%s%d%d" % (x, h, g), align_bytes=64) for x in "drf" for h, g in pieces}
+
+        pieces = [(x, h, g) for x in "drf" for h in range(2) for g in range(2)]
+        raw = {pc: sb.tile([P, PACK, HALF], BF16, name="raw_%s%d%d" % pc) for pc in pieces if pc[0] != "f"}
+        grouped = {pc: sb.tile([P, HALF, PACK], BF16, name="grouped_%s%d%d" % pc, align_bytes=64) for pc in pieces}
+        codes = {pc: sb.tile([P, HALF], U32, name="codes_%s%d%d" % pc, align_bytes=64) for pc in pieces}
+        scales = {pc: sb.tile([P, HALF], U8, name="scales_%s%d%d" % pc, align_bytes=64) for pc in pieces}
         g_codes = [sb.tile([P, N], U32, name="g_codes%d" % g, align_bytes=64) for g in range(2)]
-        warm = sb.tile([P, 8], F32, name="warm")
-        g_plane = sb.tile([P, 2, N], U8, name="g_plane", align_bytes=64)
-        f_raw = [sb.tile([P, N], BF16, name="f_raw%d" % m) for m in range(2)]
-        f_raw2 = [sb.tile([P, 2, N], BF16, name="f_pair%d" % m) for m in range(3)]
-        w_sb = [sb.tile([P, TILES, N], BF16, name="w_sb%d" % h) for h in range(2)]
-        t_sb = {q: sb.tile([P, TILES, H], F32, name="t_sb%s" % q) for q in ("00", "01", "11")}
-        a_sb = {q: sb.tile([P, TILES, H], F32, name="a_sb%s" % q) for q in ("00", "11")}
-        o_sb = {q: sb.tile([P, TILES, H], F32, name="o_sb%s" % q) for q in ("00", "01", "10", "11")}
+        g_scale_tile = sb.tile([P, 2, N], U8, name="g_scale_tile", align_bytes=64)
+        f_rows = [sb.tile([P, 2, N], BF16, name="f_rows%d" % q) for q in range(N // QUARTER)]
+        w_rows = [sb.tile([P, TILES, N], BF16, name="w_rows%d" % h) for h in range(2)]
+        sums = {quad: sb.tile([P, TILES, HALF], F32, name="sums" + quad) for quad in ("00", "01", "11")}
+        diff = {quad: sb.tile([P, TILES, HALF], F32, name="diff" + quad) for quad in ("00", "11")}
+        result = {quad: sb.tile([P, TILES, HALF], F32, name="result" + quad) for quad in ("00", "01", "10", "11")}
 
-        def f_rows(m):
-            return f_raw[m][:] if m < 2 else f_raw2[m // 2 - 1][:, m % 2, :]
+        def load_f(q):
+            rows = f[q * QUARTER:(q + 1) * QUARTER, :]
+            nc.sync.dma_start(out=f_rows[q][:], in_=rows.rearrange("(p a) l -> p a l", a=2))
 
-        def load_f(m):
-            if m < 2:
-                nc.sync.dma_start(out=f_raw[m][:], in_=f[m * P:(m + 1) * P, :])
-            else:
-                nc.sync.dma_start(out=f_raw2[m // 2 - 1][:], in_=f[m * P:(m + 2) * P, :].rearrange("(a p) l -> p a l", p=P))
-
-        def load_x(x, h, g, c0=0, c1=H):
-            nc.sync.dma_start(out=raw[x, h, g][:, :, c0:c1], in_=src[x][g * KP:(g + 1) * KP, h * H + c0:h * H + c1].rearrange("(p t) c -> p t c", t=PACK))
+        def load_piece(x, h, g):
+            rows = {"d": d, "r": r}[x][g * GROUP:(g + 1) * GROUP, h * HALF:(h + 1) * HALF]
+            nc.sync.dma_start(out=raw[x, h, g][:], in_=rows.rearrange("(p t) c -> p t c", t=PACK))
 
         def load_g(g):
-            nc.sync.dma_start(out=g_codes[g][:].bitcast(I32), in_=g_words[g].rearrange("p n t -> p (n t)").bitcast(I32))
+            words = g_words[g].rearrange("p n t -> p (n t)")
+            nc.sync.dma_start(out=g_codes[g][:].bitcast(I32), in_=words.bitcast(I32))
 
         def load_g_scales():
-            nc.vector.memset(g_plane[:].rearrange("p g n -> p (g n)").bitcast(I32), 0)
-            for q in range(4):
-                nc.gpsimd.dma_start(out=g_plane[32 * q:32 * q + 4, :, :].bitcast(I32), in_=g_scales[:, 4 * q:4 * q + 4, :].rearrange("g r n -> r g n").bitcast(I32))
-            nc.vector.memset(warm[:, 0:1], 0.0)
-            nc.scalar.mul(out=warm[:, 1:2], in_=warm[:, 0:1], mul=-1.0)
+            vector.memset(g_scale_tile[:].rearrange("p g n -> p (g n)").bitcast(I32), 0)
+            for quadrant in range(4):
+                rows = g_scales[:, 4 * quadrant:4 * quadrant + 4, :].rearrange("g q n -> q g n")
+                gpsimd.dma_start(out=g_scale_tile[32 * quadrant:32 * quadrant + 4, :, :].bitcast(I32), in_=rows.bitcast(I32))
 
         def load_w(h):
-            nc.sync.dma_start(out=w_sb[h][:], in_=w[h * H:(h + 1) * H, :].rearrange("(a p) j -> p a j", p=P))
+            rows = w[h * HALF:(h + 1) * HALF, :]
+            nc.sync.dma_start(out=w_rows[h][:], in_=rows.rearrange("(a p) j -> p a j", p=P))
 
-        def turn_f(m, k0):
-            words = f_rows(m).bitcast(F32)
-            for g in range(2):
+        def f_bank(q, g):
+            return bank[TILES + (2 * q + g) % TILES]
+
+        def transpose_f(q, g):
+            words = f_rows[q][:].bitcast(F32)
+            for a in range(2):
                 for u in range(2):
-                    k = 2 * g + u
-                    nc.tensor.transpose(bank[k0][:, k * P:(k + 1) * P], words[:, 256 * g + u:256 * (g + 1):2], ident[:])
+                    slot = 2 * a + u
+                    nc.tensor.transpose(f_bank(q, g)[:, slot * P:(slot + 1) * P],
+                                        words[:, a, g * GROUP // 2 + u:(g + 1) * GROUP // 2:2], ident[:])
 
-        def unload_f(m, k0):
-            h, a = divmod(m, TILES)
-            dst = f_grouped[h][:, :, a * P:(a + 1) * P, :].bitcast(F32)
-            nc.scalar.copy(out=dst, in_=bank[k0][:].rearrange("p (g u i) -> p g i u", g=2, u=2))
+        def unload_f(q, g):
+            h, c0 = divmod(q * QUARTER, HALF)
+            words = grouped["f", h, g][:, c0:c0 + QUARTER, :].bitcast(F32)
+            scalar.copy(out=words.rearrange("p (m a) u -> p m a u", a=2),
+                        in_=f_bank(q, g)[:].rearrange("p (a u m) -> p m a u", a=2, u=2))
 
-        def group(eng, x, h, g, c0, c1):
+        def interleave(engine, x, h, g, c0, c1):
             dst = grouped[x, h, g][:, c0:c1, :].rearrange("p (c i) t -> p c t i", i=4)
-            s = raw[x, h, g][:, :, c0:c1].rearrange("p t (c i) -> p c t i", i=4)
-            if eng == "V":
-                if h == 0:
-                    nc.vector.tensor_scalar_mul(out=dst, in0=s, scalar1=-1.0)
-                else:
-                    nc.vector.tensor_copy(out=dst, in_=s)
+            src = raw[x, h, g][:, :, c0:c1].rearrange("p t (c i) -> p c t i", i=4)
+            if engine == "vector" and h == 0:
+                vector.tensor_scalar_mul(out=dst, in0=src, scalar1=-1.0)
+            elif engine == "vector":
+                vector.tensor_copy(out=dst, in_=src)
             elif h == 0:
-                nc.scalar.mul(out=dst, in_=s, mul=-1.0)
+                scalar.mul(out=dst, in_=src, mul=-1.0)
             else:
-                nc.scalar.copy(out=dst, in_=s)
+                scalar.copy(out=dst, in_=src)
 
-        def quant(x, h, g, c0=0, c1=H):
-            values = f_grouped[h][:, g, c0:c1, :] if x == "f" else grouped[x, h, g][:, c0:c1, :]
-            nc.vector.quantize_mx(out=codes[x, h, g][:, c0:c1].bitcast(E4M3), scales=scales[x, h, g][:, c0:c1],
-                                  in_=values.rearrange("p c t -> p (c t)"))
+        def quantize(x, h, g, c0=0, c1=HALF):
+            vector.quantize_mx(out=codes[x, h, g][:, c0:c1].bitcast(E4M3), scales=scales[x, h, g][:, c0:c1],
+                               in_=grouped[x, h, g][:, c0:c1, :].rearrange("p c t -> p (c t)"))
 
-        def operand(x, h, g, c0, c1):
+        def quantize_f(q, g):
+            h, c0 = divmod(q * QUARTER, HALF)
+            quantize("f", h, g, c0, c0 + QUARTER)
+
+        def operand(name, g, c0, c1):
+            x, h = name[0], int(name[1])
             if x == "G":
-                return g_codes[g][:, h * H + c0:h * H + c1].bitcast(E5M2), g_plane[:, g, h * H + c0:h * H + c1]
+                cols = slice(h * HALF + c0, h * HALF + c1)
+                return g_codes[g][:, cols].bitcast(E5M2), g_scale_tile[:, g, cols]
             return codes[x, h, g][:, c0:c1].bitcast(E4M3), scales[x, h, g][:, c0:c1]
 
-        def mx(k, a, stat, mov, g, start=False, stop=False):
-            lhs, lhs_scale = operand(stat[0], int(stat[1]), g, a * P, (a + 1) * P)
-            rhs, rhs_scale = operand(mov[0], int(mov[1]), g, 0, H)
-            nc.tensor.matmul_mx(out=bank[k][:], lhsT=lhs, lhsT_scale=lhs_scale, rhs=rhs, rhs_scale=rhs_scale, start=start, stop=stop)
+        passes_done = {}
 
-        def mx4(k0, stat, mov, g, start=False, stop=False):
-            for a in range(TILES):
-                mx(k0 + a, a, stat, mov, g, start, stop)
+        def multiply(quad, stationary, moving, groups, tiles):
+            for g in groups:
+                for a in range(*tiles):
+                    done = passes_done.get((quad, a), 0)
+                    passes_done[quad, a] = done + 1
+                    lhs, lhs_scale = operand(stationary, g, a * P, (a + 1) * P)
+                    rhs, rhs_scale = operand(moving, g, 0, HALF)
+                    nc.tensor.matmul_mx(out=bank[FIRST_BANK[quad] + a][:], lhsT=lhs, lhsT_scale=lhs_scale, rhs=rhs,
+                                        rhs_scale=rhs_scale, start=done == 0, stop=done == PASSES[quad] - 1)
 
-        def unload_t(q, k, a, b0=0, b1=TILES):
-            cols = slice(b0 * P, b1 * P)
-            if q == "01":
-                nc.scalar.mul(out=t_sb[q][:, a, cols], in_=bank[k][:, cols], mul=-1.0)
+        def unload(quad, a):
+            if quad == "01":
+                scalar.mul(out=sums[quad][:, a, :], in_=bank[FIRST_BANK[quad] + a][:], mul=-1.0)
             else:
-                nc.scalar.copy(out=t_sb[q][:, a, cols], in_=bank[k][:, cols])
-
-        def turn(k, slot, q, a, b):
-            nc.tensor.transpose(bank[k][:, slot * P:(slot + 1) * P], t_sb[q][:, a, b * P:(b + 1) * P], ident[:])
-
-        def turn_box(q, k, rows, cols):
-            slot = 0
-            for a in range(*rows):
-                for b in range(*cols):
-                    turn(k, slot, q, b, a)
-                    slot += 1
-
-        def turn_row(q, k, a, n):
-            turn_box(q, k, (a, a + 1), (0, n))
-
-        def turn_col(q, k, b):
-            turn_box(q, k, (0, 4), (b, b + 1))
+                scalar.copy(out=sums[quad][:, a, :], in_=bank[FIRST_BANK[quad] + a][:])
 
         def blocks(tile, rows, cols):
             return tile[:, rows[0]:rows[1], cols[0] * P:cols[1] * P]
 
-        def bank_as(k, rows, cols, s0=0):
-            n = (rows[1] - rows[0]) * (cols[1] - cols[0])
-            return bank[k][:, s0 * P:(s0 + n) * P].rearrange("p (a c) -> p a c", a=rows[1] - rows[0])
+        def in_bank(k, rows, cols, slot=0):
+            count = (rows[1] - rows[0]) * (cols[1] - cols[0])
+            return bank[k][:, slot * P:(slot + count) * P].rearrange("p (a c) -> p a c", a=rows[1] - rows[0])
 
-        def sub(q, k, rows, cols, s0=0):
-            t, tt = blocks(t_sb[q], rows, cols), bank_as(k, rows, cols, s0)
-            nc.vector.tensor_tensor(out=blocks(a_sb[q], rows, cols), in0=t, in1=tt, op=SUB)
+        def transpose_sums(quad, k, rows, cols):
+            slot = 0
+            for a in range(*rows):
+                for b in range(*cols):
+                    nc.tensor.transpose(bank[k][:, slot * P:(slot + 1) * P], sums[quad][:, b, a * P:(a + 1) * P], ident[:])
+                    slot += 1
 
-        def w_blocks(q, rows, cols):
-            c = int(q[1]) * TILES
-            return blocks(w_sb[int(q[0])], rows, (cols[0] + c, cols[1] + c))
+        def subtract(quad, k, rows, cols, slot=0):
+            vector.tensor_tensor(out=blocks(diff[quad], rows, cols), in0=blocks(sums[quad], rows, cols),
+                                 in1=in_bank(k, rows, cols, slot), op=SUB)
 
-        def weigh(q, rows, cols, k=None, eng=None):
-            a = blocks(a_sb[q], rows, cols) if k is None else bank_as(k, rows, cols)
-            (eng or nc.vector).tensor_tensor(out=blocks(o_sb[q], rows, cols), in0=a, in1=w_blocks(q, rows, cols), op=MULT)
+        def weigh(engine, quad, rows, cols):
+            src = blocks(diff[quad], rows, cols) if quad in diff else in_bank(TILES + rows[0], rows, cols)
+            first = int(quad[1]) * TILES
+            weight = blocks(w_rows[int(quad[0])], rows, (first + cols[0], first + cols[1]))
+            engine.tensor_tensor(out=blocks(result[quad], rows, cols), in0=src, in1=weight, op=MULT)
 
-        def store(q, rows, cols):
-            r0, c0 = int(q[0]) * H, int(q[1]) * H
-            dst = out[r0 + rows[0] * P:r0 + rows[1] * P, c0 + cols[0] * P:c0 + cols[1] * P].rearrange("(a p) j -> p a j", p=P)
-            nc.sync.dma_start(out=dst, in_=blocks(o_sb[q], rows, cols))
+        def store(quad, rows, cols):
+            i0, j0 = int(quad[0]) * HALF, int(quad[1]) * HALF
+            dst = out[i0 + rows[0] * P:i0 + rows[1] * P, j0 + cols[0] * P:j0 + cols[1] * P]
+            nc.sync.dma_start(out=dst.rearrange("(a p) j -> p a j", p=P), in_=blocks(result[quad], rows, cols))
+
+        def row(a):
+            return (a, a + 1)
 
         with tc.manual_schedule():
-            make_identity(nc, ident[:])
+            make_identity(nc, ident_bf16[:])
+            scalar.copy(out=ident[:], in_=ident_bf16[:])
+
             load_f(0)
             load_g_scales()
             load_f(1)
+            load_piece("r", 0, 0)
             load_f(2)
-            load_x("r", 0, 0)
-            load_f(4)
-            load_f(6)
-            load_x("d", 0, 0)
-            load_g(0)
-            turn_f(0, 4)
-            turn_f(1, 5)
-            turn_f(2, 6)
-            turn_f(3, 7)
-            unload_f(0, 4)
-            load_x("r", 0, 1)
-            load_x("d", 0, 1)
-            unload_f(1, 5)
-            quant("f", 0, 1, 0, 256)
-            load_x("r", 1, 0)
-            group("V", "r", 0, 0, 0, 256)
-            quant("f", 0, 0, 0, 256)
-            quant("r", 0, 0, 0, 256)
-            unload_f(2, 6)
-            turn_f(4, 4)
-            load_g(1)
-            load_x("d", 1, 0)
-            load_x("d", 1, 1)
-            load_x("r", 1, 1)
-            turn_f(5, 5)
-            unload_f(3, 7)
-            quant("f", 0, 0, 256, 512)
-            mx(0, 0, "r0", "f0", 0, start=True)
-            mx(1, 1, "r0", "f0", 0, start=True)
-            unload_f(4, 4)
-            unload_f(5, 5)
-            group("S", "d", 0, 0, 160, 256)
-            group("V", "r", 0, 0, 256, 512)
-            quant("f", 0, 1, 256, 512)
-            quant("r", 0, 0, 256, 512)
-            turn_f(6, 6)
-            group("S", "d", 0, 0, 384, 512)
-            unload_f(6, 6)
-            group("V", "d", 0, 0, 0, 160)
-            load_w(0)
-            turn_f(7, 7)
-            mx(2, 2, "r0", "f0", 0, start=True)
-            mx(3, 3, "r0", "f0", 0, start=True)
-            quant("d", 0, 0, 0, 256)
-            unload_f(7, 7)
-            group("V", "d", 0, 0, 256, 384)
-            quant("f", 1, 0, 0, 256)
-            quant("d", 0, 0, 256, 512)
-            quant("f", 1, 1, 0, 256)
-            quant("f", 1, 1, 256, 512)
-            quant("f", 1, 0, 256, 512)
-            mx(0, 0, "d0", "G0", 0)
-            mx(1, 1, "d0", "G0", 0)
-            mx(4, 0, "d0", "G1", 0, start=True)
-            mx(5, 1, "d0", "G1", 0, start=True)
-            mx(2, 2, "d0", "G0", 0)
-            mx(3, 3, "d0", "G0", 0)
-            group("V", "r", 0, 1, 256, 512)
-            group("S", "r", 0, 1, 0, 256)
-            group("S", "d", 0, 1, 0, 256)
-            quant("r", 0, 1, 0, 256)
-            quant("r", 0, 1, 256, 512)
-            mx(6, 2, "d0", "G1", 0, start=True)
-            mx(7, 3, "d0", "G1", 0, start=True)
-            group("S", "r", 1, 0, 192, 512)
-            mx(4, 0, "r0", "f1", 0)
-            mx(5, 1, "r0", "f1", 0)
-            mx(6, 2, "r0", "f1", 0)
-            mx(7, 3, "r0", "f1", 0)
-            mx(4, 0, "r0", "f1", 1)
-            mx(5, 1, "r0", "f1", 1)
-            group("V", "d", 0, 1, 256, 512)
-            quant("d", 0, 1, 0, 256)
-            quant("d", 0, 1, 256, 512)
-            group("V", "r", 1, 0, 0, 192)
-            quant("r", 1, 0, 0, 512)
-            group("V", "d", 1, 0, 0, 512)
-            group("V", "d", 1, 1, 0, 512)
-            mx(0, 0, "r0", "f0", 1)
-            mx(1, 1, "r0", "f0", 1)
-            mx(2, 2, "r0", "f0", 1)
-            mx(3, 3, "r0", "f0", 1)
-            mx(0, 0, "d0", "G0", 1, stop=True)
-            mx(1, 1, "d0", "G0", 1, stop=True)
-            mx(2, 2, "d0", "G0", 1, stop=True)
-            mx(3, 3, "d0", "G0", 1, stop=True)
-            quant("d", 1, 0, 0, 512)
-            unload_t("00", 0, 0)
-            unload_t("00", 1, 1)
-            mx(4, 0, "d0", "G1", 1)
-            mx(5, 1, "d0", "G1", 1)
-            mx(6, 2, "r0", "f1", 1)
-            mx(7, 3, "r0", "f1", 1)
-            mx(6, 2, "d0", "G1", 1)
-            mx(7, 3, "d0", "G1", 1)
-            unload_t("00", 2, 2)
-            unload_t("00", 3, 3)
-            group("S", "r", 1, 1, 128, 512)
-            mx(4, 0, "f0", "r1", 0)
-            mx(5, 1, "f0", "r1", 0)
-            mx(6, 2, "f0", "r1", 0)
-            mx(7, 3, "f0", "r1", 0)
-            turn_row("00", 0, 0, 4)
-            turn_row("00", 1, 1, 4)
-            turn_row("00", 2, 2, 4)
-            turn_row("00", 3, 3, 4)
-            mx(4, 0, "G0", "d1", 0)
-            mx(5, 1, "G0", "d1", 0)
-            mx(6, 2, "G0", "d1", 0)
-            mx(7, 3, "G0", "d1", 0)
-            group("V", "r", 1, 1, 0, 128)
-            quant("d", 1, 1, 0, 512)
-            sub("00", 0, (0, 1), (0, 4))
-            quant("r", 1, 1, 0, 512)
-            sub("00", 1, (1, 2), (0, 4))
-            sub("00", 2, (2, 3), (0, 4))
-            mx(4, 0, "G0", "d1", 1)
-            mx(5, 1, "G0", "d1", 1)
-            mx(6, 2, "G0", "d1", 1)
-            mx(7, 3, "G0", "d1", 1)
-            weigh("00", (0, 1), (0, 4), eng=nc.gpsimd)
-            mx(4, 0, "f0", "r1", 1, stop=True)
-            mx(5, 1, "f0", "r1", 1, stop=True)
-            mx(6, 2, "f0", "r1", 1, stop=True)
-            mx(7, 3, "f0", "r1", 1, stop=True)
-            unload_t("01", 4, 0)
-            unload_t("01", 5, 1)
-            mx(0, 0, "G1", "d1", 0, start=True)
-            mx(0, 0, "G1", "d1", 1)
-            mx(1, 1, "G1", "d1", 0, start=True)
-            mx(1, 1, "G1", "d1", 1)
-            sub("00", 3, (3, 4), (0, 4))
-            weigh("01", (0, 1), (0, 4), k=4)
-            weigh("01", (1, 2), (0, 4), k=5)
-            unload_t("01", 6, 2)
-            mx(0, 0, "f1", "r1", 0)
-            mx(0, 0, "f1", "r1", 1, stop=True)
-            mx(1, 1, "f1", "r1", 0)
-            mx(1, 1, "f1", "r1", 1, stop=True)
-            unload_t("01", 7, 3)
-            unload_t("11", 0, 0)
-            unload_t("11", 1, 1)
-            mx(2, 2, "G1", "d1", 0, start=True)
-            mx(2, 2, "G1", "d1", 1)
-            turn_row("01", 4, 0, 4)
-            weigh("00", (1, 2), (0, 4), eng=nc.gpsimd)
-            mx(2, 2, "f1", "r1", 0)
-            mx(2, 2, "f1", "r1", 1, stop=True)
-            load_w(1)
-            weigh("00", (2, 3), (0, 4), eng=nc.gpsimd)
-            turn_box("11", 0, (0, 2), (0, 2))
-            store("00", (0, 2), (0, 4))
-            weigh("01", (2, 3), (0, 4), k=6)
-            weigh("01", (3, 4), (0, 4), k=7)
-            turn_row("01", 5, 1, 4)
-            turn_row("01", 6, 2, 4)
-            turn_row("01", 7, 3, 4)
-            unload_t("11", 2, 2)
-            turn_col("11", 2, 2)
-            weigh("10", (0, 1), (0, 4), k=4)
-            sub("11", 0, (0, 2), (0, 2), 0)
-            weigh("10", (1, 2), (0, 4), k=5)
-            weigh("00", (3, 4), (0, 4), eng=nc.gpsimd)
-            weigh("11", (0, 2), (0, 2), eng=nc.gpsimd)
-            weigh("10", (2, 3), (0, 4), k=6)
-            mx(3, 3, "f1", "r1", 0, start=True)
-            mx(3, 3, "f1", "r1", 1)
-            mx(3, 3, "G1", "d1", 0)
-            mx(3, 3, "G1", "d1", 1, stop=True)
-            turn_box("11", 1, (2, 4), (0, 2))
-            unload_t("11", 3, 3, 0, 2)
-            store("01", (0, 2), (0, 4))
-            unload_t("11", 3, 3, 2, 4)
-            turn_box("11", 0, (0, 2), (3, 4))
-            turn_box("11", 3, (2, 4), (3, 4))
-            sub("11", 2, (0, 3), (2, 3), 0)
-            weigh("10", (3, 4), (0, 4), k=7)
-            sub("11", 1, (2, 3), (0, 2), 0)
-            weigh("11", (0, 3), (2, 3), eng=nc.gpsimd)
-            weigh("11", (2, 3), (0, 2), eng=nc.gpsimd)
-            sub("11", 1, (3, 4), (0, 2), 2)
-            store("01", (2, 4), (0, 4))
-            store("00", (2, 4), (0, 4))
-            store("10", (0, 2), (0, 4))
-            store("10", (2, 4), (0, 4))
-            sub("11", 2, (3, 4), (2, 3), 3)
-            sub("11", 0, (0, 2), (3, 4), 0)
-            weigh("11", (3, 4), (0, 3))
-            sub("11", 3, (2, 4), (3, 4), 0)
-            weigh("11", (0, 2), (3, 4))
+            load_piece("r", 0, 1)
+            load_f(3)
+            for g in range(2):
+                load_piece("d", 0, g)
+            for g in range(2):
+                load_g(g)
+            for x, g in (("d", 0), ("r", 0), ("r", 1), ("d", 1)):
+                load_piece(x, 1, g)
+            for h in range(2):
+                load_w(h)
+
+            for q in range(2):
+                for g in range(2):
+                    transpose_f(q, g)
+            unload_f(0, 0)
+            unload_f(0, 1)
+            quantize_f(0, 0)
+            unload_f(1, 0)
+            interleave("vector", "r", 0, 0, 0, 192)
+            interleave("scalar", "r", 0, 0, 192, QUARTER)
+            unload_f(1, 1)
+            quantize_f(1, 0)
+            quantize("r", 0, 0, 0, QUARTER)
+            transpose_f(2, 0)
+            quantize_f(0, 1)
+            interleave("vector", "r", 0, 0, QUARTER, HALF)
+            multiply("00", "r0", "f0", [0], (0, 2))
+            unload_f(2, 0)
+            quantize("r", 0, 0, QUARTER, HALF)
+            interleave("scalar", "r", 0, 1, QUARTER, HALF)
+            quantize_f(2, 0)
+            transpose_f(2, 1)
+            quantize_f(1, 1)
+            interleave("vector", "r", 0, 1, 0, QUARTER)
+            transpose_f(3, 0)
+            transpose_f(3, 1)
+            unload_f(2, 1)
+            unload_f(3, 0)
+            unload_f(3, 1)
+            quantize("r", 0, 1, 0, QUARTER)
+            quantize("r", 0, 1, QUARTER, HALF)
+            multiply("00", "r0", "f0", [0], (2, 4))
+            multiply("00", "r0", "f0", [1], ALL)
+            quantize_f(2, 1)
+            quantize_f(3, 0)
+            multiply("01", "r0", "f1", [0], ALL)
+
+            interleave("scalar", "d", 0, 0, QUARTER, HALF)
+            interleave("vector", "d", 0, 0, 0, QUARTER)
+            quantize_f(3, 1)
+            multiply("01", "r0", "f1", [1], ALL)
+            quantize("d", 0, 0, 0, QUARTER)
+            interleave("scalar", "d", 0, 1, QUARTER, HALF)
+            interleave("vector", "d", 0, 1, 0, QUARTER)
+            quantize("d", 0, 0, QUARTER, HALF)
+            quantize("d", 0, 1, 0, QUARTER)
+            quantize("d", 0, 1, QUARTER, HALF)
+            multiply("00", "d0", "G0", [0, 1], ALL)
+            multiply("01", "d0", "G1", [0, 1], ALL)
+
+            interleave("vector", "d", 1, 0, 0, 352)
+            interleave("scalar", "d", 1, 0, 352, HALF)
+            for a in range(TILES):
+                unload("00", a)
+            quantize("d", 1, 0)
+            multiply("01", "G0", "d1", [0], ALL)
+            interleave("vector", "r", 1, 0, 0, HALF)
+            interleave("vector", "r", 1, 1, 0, 288)
+            interleave("scalar", "r", 1, 1, 288, HALF)
+            quantize("r", 1, 0)
+            for a in range(TILES):
+                transpose_sums("00", a, row(a), ALL)
+            interleave("scalar", "d", 1, 1, 160, HALF)
+            quantize("r", 1, 1)
+            multiply("01", "f0", "r1", [0, 1], ALL)
+            interleave("vector", "d", 1, 1, 0, 160)
+            subtract("00", 0, row(0), ALL)
+            quantize("d", 1, 1)
+            multiply("01", "G0", "d1", [1], ALL)
+            for a in range(1, TILES):
+                subtract("00", a, row(a), ALL)
+            for a in range(TILES):
+                weigh(gpsimd, "00", row(a), ALL)
+            store("00", row(0), ALL)
+            store("00", row(1), ALL)
+            for a in range(TILES):
+                unload("01", a)
+                weigh(vector, "01", row(a), ALL)
+                store("01", row(a), ALL)
+            store("00", row(2), ALL)
+            store("00", row(3), ALL)
+
+            for stationary, moving in (("G1", "d1"), ("f1", "r1")):
+                for a in range(2):
+                    multiply("11", stationary, moving, [0, 1], row(a))
+            multiply("11", "f1", "r1", [0, 1], row(2))
+            multiply("11", "G1", "d1", [0, 1], row(2))
+            for a in range(3):
+                unload("11", a)
+            transpose_sums("01", TILES, row(0), ALL)
+            transpose_sums("11", 0, (0, 2), (0, 2))
+            transpose_sums("01", TILES + 1, row(1), ALL)
+            transpose_sums("01", TILES + 2, row(2), ALL)
+            transpose_sums("11", 2, ALL, (2, 3))
+            multiply("11", "G1", "d1", [0, 1], row(3))
+            multiply("11", "f1", "r1", [0, 1], row(3))
+            unload("11", 3)
+            transpose_sums("01", TILES + 3, row(3), ALL)
+            transpose_sums("11", 1, (2, 4), (0, 2))
+            transpose_sums("11", 3, ALL, (3, 4))
+
+            weigh(vector, "10", row(0), ALL)
+            subtract("11", 0, (0, 2), (0, 2))
+            weigh(gpsimd, "11", (0, 2), (0, 2))
+            weigh(vector, "10", row(1), ALL)
+            subtract("11", 2, (0, 3), (2, 3))
+            weigh(gpsimd, "11", (0, 3), (2, 3))
+            weigh(vector, "10", row(2), ALL)
+            weigh(vector, "10", row(3), ALL)
+            for a in range(TILES):
+                store("10", row(a), ALL)
             store("11", (0, 2), (0, 3))
-            weigh("11", (2, 4), (3, 4))
-            store("11", (2, 4), (0, 3))
-            store("11", (0, 2), (3, 4))
-            store("11", (2, 4), (3, 4))
+            subtract("11", 1, row(2), (0, 2))
+            weigh(gpsimd, "11", row(2), (0, 2))
+            store("11", row(2), (0, 3))
+            subtract("11", 2, row(3), (2, 3), slot=3)
+            subtract("11", 3, ALL, (3, 4))
+            subtract("11", 1, row(3), (0, 2), slot=2)
+            weigh(vector, "11", ALL, (3, 4))
+            store("11", (0, 3), (3, 4))
+            weigh(vector, "11", row(3), (0, 3))
+            store("11", row(3), ALL)

from contextlib import ExitStack

import concourse.mybir as mybir
from concourse.masks import make_identity

N = 1024
FLOPS = 4 * N * N * N

F32 = mybir.dt.float32
BF16 = mybir.dt.bfloat16
I32 = mybir.dt.int32
U32 = mybir.dt.uint32
U8 = mybir.dt.uint8
E4M3 = mybir.dt.float8_e4m3fn_x4
E5M2 = mybir.dt.float8_e5m2_x4
MULT = mybir.AluOpType.mult
SUB = mybir.AluOpType.subtract

P = 128
PACK = 4
GROUP = P * PACK
HALF = N // 2
QUARTER = N // 4
TILES = HALF // P
ALL = (0, TILES)
FIRST_BANK = {"00": 0, "11": 0, "01": TILES}
PASSES = {"00": 4, "11": 4, "01": 8}


def tile_commutator_directional_derivative_e4_kernel(tc, g_words, g_scales, d, f, r, w, out):
    nc = tc.nc
    vector, scalar, gpsimd = nc.vector, nc.scalar, nc.gpsimd
    with ExitStack() as ctx:
        sb = ctx.enter_context(tc.tile_pool(name="sb", bufs=1))
        ps = ctx.enter_context(tc.psum_pool(name="ps", bufs=1))
        bank = [ps.tile([P, HALF], F32, name="bank%d" % k) for k in range(2 * TILES)]
        ident_bf16 = sb.tile([P, P], BF16, name="ident_bf16")
        ident = sb.tile([P, P], F32, name="ident")

        pieces = [(x, h, g) for x in "drf" for h in range(2) for g in range(2)]
        raw = {pc: sb.tile([P, PACK, HALF], BF16, name="raw_%s%d%d" % pc) for pc in pieces if pc[0] != "f"}
        grouped = {pc: sb.tile([P, HALF, PACK], BF16, name="grouped_%s%d%d" % pc, align_bytes=64) for pc in pieces}
        codes = {pc: sb.tile([P, HALF], U32, name="codes_%s%d%d" % pc, align_bytes=64) for pc in pieces}
        scales = {pc: sb.tile([P, HALF], U8, name="scales_%s%d%d" % pc, align_bytes=64) for pc in pieces}
        g_codes = [sb.tile([P, N], U32, name="g_codes%d" % g, align_bytes=64) for g in range(2)]
        g_scale_tile = sb.tile([P, 2, N], U8, name="g_scale_tile", align_bytes=64)
        f_rows = [sb.tile([P, 2, N], BF16, name="f_rows%d" % q) for q in range(N // QUARTER)]
        w_rows = [sb.tile([P, TILES, N], BF16, name="w_rows%d" % h) for h in range(2)]
        sums = {quad: sb.tile([P, TILES, HALF], F32, name="sums" + quad) for quad in ("00", "01", "11")}
        diff = {quad: sb.tile([P, TILES, HALF], F32, name="diff" + quad) for quad in ("00", "11")}
        result = {quad: sb.tile([P, TILES, HALF], F32, name="result" + quad) for quad in ("00", "01", "10", "11")}

        def load_f(q):
            rows = f[q * QUARTER:(q + 1) * QUARTER, :]
            nc.sync.dma_start(out=f_rows[q][:], in_=rows.rearrange("(p a) l -> p a l", a=2))

        def load_piece(x, h, g):
            rows = {"d": d, "r": r}[x][g * GROUP:(g + 1) * GROUP, h * HALF:(h + 1) * HALF]
            nc.sync.dma_start(out=raw[x, h, g][:], in_=rows.rearrange("(p t) c -> p t c", t=PACK))

        def load_g(g):
            words = g_words[g].rearrange("p n t -> p (n t)")
            nc.sync.dma_start(out=g_codes[g][:].bitcast(I32), in_=words.bitcast(I32))

        def load_g_scales():
            vector.memset(g_scale_tile[:].rearrange("p g n -> p (g n)").bitcast(I32), 0)
            for quadrant in range(4):
                rows = g_scales[:, 4 * quadrant:4 * quadrant + 4, :].rearrange("g q n -> q g n")
                gpsimd.dma_start(out=g_scale_tile[32 * quadrant:32 * quadrant + 4, :, :].bitcast(I32), in_=rows.bitcast(I32))

        def load_w(h):
            rows = w[h * HALF:(h + 1) * HALF, :]
            nc.sync.dma_start(out=w_rows[h][:], in_=rows.rearrange("(a p) j -> p a j", p=P))

        def f_bank(q, g):
            return bank[TILES + (2 * q + g) % TILES]

        def transpose_f(q, g):
            words = f_rows[q][:].bitcast(F32)
            for a in range(2):
                for u in range(2):
                    slot = 2 * a + u
                    nc.tensor.transpose(f_bank(q, g)[:, slot * P:(slot + 1) * P],
                                        words[:, a, g * GROUP // 2 + u:(g + 1) * GROUP // 2:2], ident[:])

        def unload_f(q, g):
            h, c0 = divmod(q * QUARTER, HALF)
            words = grouped["f", h, g][:, c0:c0 + QUARTER, :].bitcast(F32)
            scalar.copy(out=words.rearrange("p (m a) u -> p m a u", a=2),
                        in_=f_bank(q, g)[:].rearrange("p (a u m) -> p m a u", a=2, u=2))

        def interleave(engine, x, h, g, c0, c1):
            dst = grouped[x, h, g][:, c0:c1, :].rearrange("p (c i) t -> p c t i", i=4)
            src = raw[x, h, g][:, :, c0:c1].rearrange("p t (c i) -> p c t i", i=4)
            if engine == "vector" and h == 0:
                vector.tensor_scalar_mul(out=dst, in0=src, scalar1=-1.0)
            elif engine == "vector":
                vector.tensor_copy(out=dst, in_=src)
            elif h == 0:
                scalar.mul(out=dst, in_=src, mul=-1.0)
            else:
                scalar.copy(out=dst, in_=src)

        def quantize(x, h, g, c0=0, c1=HALF):
            vector.quantize_mx(out=codes[x, h, g][:, c0:c1].bitcast(E4M3), scales=scales[x, h, g][:, c0:c1],
                               in_=grouped[x, h, g][:, c0:c1, :].rearrange("p c t -> p (c t)"))

        def quantize_f(q, g):
            h, c0 = divmod(q * QUARTER, HALF)
            quantize("f", h, g, c0, c0 + QUARTER)

        def operand(name, g, c0, c1):
            x, h = name[0], int(name[1])
            if x == "G":
                cols = slice(h * HALF + c0, h * HALF + c1)
                return g_codes[g][:, cols].bitcast(E5M2), g_scale_tile[:, g, cols]
            return codes[x, h, g][:, c0:c1].bitcast(E4M3), scales[x, h, g][:, c0:c1]

        passes_done = {}

        def multiply(quad, stationary, moving, groups, tiles):
            for g in groups:
                for a in range(*tiles):
                    done = passes_done.get((quad, a), 0)
                    passes_done[quad, a] = done + 1
                    lhs, lhs_scale = operand(stationary, g, a * P, (a + 1) * P)
                    rhs, rhs_scale = operand(moving, g, 0, HALF)
                    nc.tensor.matmul_mx(out=bank[FIRST_BANK[quad] + a][:], lhsT=lhs, lhsT_scale=lhs_scale, rhs=rhs,
                                        rhs_scale=rhs_scale, start=done == 0, stop=done == PASSES[quad] - 1)

        def unload(quad, a):
            if quad == "01":
                scalar.mul(out=sums[quad][:, a, :], in_=bank[FIRST_BANK[quad] + a][:], mul=-1.0)
            else:
                scalar.copy(out=sums[quad][:, a, :], in_=bank[FIRST_BANK[quad] + a][:])

        def blocks(tile, rows, cols):
            return tile[:, rows[0]:rows[1], cols[0] * P:cols[1] * P]

        def in_bank(k, rows, cols, slot=0):
            count = (rows[1] - rows[0]) * (cols[1] - cols[0])
            return bank[k][:, slot * P:(slot + count) * P].rearrange("p (a c) -> p a c", a=rows[1] - rows[0])

        def transpose_sums(quad, k, rows, cols):
            slot = 0
            for a in range(*rows):
                for b in range(*cols):
                    nc.tensor.transpose(bank[k][:, slot * P:(slot + 1) * P], sums[quad][:, b, a * P:(a + 1) * P], ident[:])
                    slot += 1

        def subtract(quad, k, rows, cols, slot=0):
            vector.tensor_tensor(out=blocks(diff[quad], rows, cols), in0=blocks(sums[quad], rows, cols),
                                 in1=in_bank(k, rows, cols, slot), op=SUB)

        def weigh(engine, quad, rows, cols):
            src = blocks(diff[quad], rows, cols) if quad in diff else in_bank(TILES + rows[0], rows, cols)
            first = int(quad[1]) * TILES
            weight = blocks(w_rows[int(quad[0])], rows, (first + cols[0], first + cols[1]))
            engine.tensor_tensor(out=blocks(result[quad], rows, cols), in0=src, in1=weight, op=MULT)

        def store(quad, rows, cols):
            i0, j0 = int(quad[0]) * HALF, int(quad[1]) * HALF
            dst = out[i0 + rows[0] * P:i0 + rows[1] * P, j0 + cols[0] * P:j0 + cols[1] * P]
            nc.sync.dma_start(out=dst.rearrange("(a p) j -> p a j", p=P), in_=blocks(result[quad], rows, cols))

        def row(a):
            return (a, a + 1)

        with tc.manual_schedule():
            make_identity(nc, ident_bf16[:])
            scalar.copy(out=ident[:], in_=ident_bf16[:])

            load_f(0)
            load_g_scales()
            load_f(1)
            load_piece("r", 0, 0)
            load_f(2)
            load_piece("r", 0, 1)
            load_f(3)
            for g in range(2):
                load_piece("d", 0, g)
            for g in range(2):
                load_g(g)
            for x, g in (("d", 0), ("r", 0), ("r", 1), ("d", 1)):
                load_piece(x, 1, g)
            for h in range(2):
                load_w(h)

            for q in range(2):
                for g in range(2):
                    transpose_f(q, g)
            unload_f(0, 0)
            unload_f(0, 1)
            quantize_f(0, 0)
            unload_f(1, 0)
            interleave("vector", "r", 0, 0, 0, 192)
            interleave("scalar", "r", 0, 0, 192, QUARTER)
            unload_f(1, 1)
            quantize_f(1, 0)
            quantize("r", 0, 0, 0, QUARTER)
            transpose_f(2, 0)
            quantize_f(0, 1)
            interleave("vector", "r", 0, 0, QUARTER, HALF)
            multiply("00", "r0", "f0", [0], (0, 2))
            unload_f(2, 0)
            quantize("r", 0, 0, QUARTER, HALF)
            interleave("scalar", "r", 0, 1, QUARTER, HALF)
            quantize_f(2, 0)
            transpose_f(2, 1)
            quantize_f(1, 1)
            interleave("vector", "r", 0, 1, 0, QUARTER)
            transpose_f(3, 0)
            transpose_f(3, 1)
            unload_f(2, 1)
            unload_f(3, 0)
            unload_f(3, 1)
            quantize("r", 0, 1, 0, QUARTER)
            quantize("r", 0, 1, QUARTER, HALF)
            multiply("00", "r0", "f0", [0], (2, 4))
            multiply("00", "r0", "f0", [1], ALL)
            quantize_f(2, 1)
            quantize_f(3, 0)
            multiply("01", "r0", "f1", [0], ALL)

            interleave("scalar", "d", 0, 0, QUARTER, HALF)
            interleave("vector", "d", 0, 0, 0, QUARTER)
            quantize_f(3, 1)
            multiply("01", "r0", "f1", [1], ALL)
            quantize("d", 0, 0, 0, QUARTER)
            interleave("scalar", "d", 0, 1, QUARTER, HALF)
            interleave("vector", "d", 0, 1, 0, QUARTER)
            quantize("d", 0, 0, QUARTER, HALF)
            quantize("d", 0, 1, 0, QUARTER)
            quantize("d", 0, 1, QUARTER, HALF)
            multiply("00", "d0", "G0", [0, 1], ALL)
            multiply("01", "d0", "G1", [0, 1], ALL)

            interleave("vector", "d", 1, 0, 0, 352)
            interleave("scalar", "d", 1, 0, 352, HALF)
            for a in range(TILES):
                unload("00", a)
            quantize("d", 1, 0)
            multiply("01", "G0", "d1", [0], ALL)
            interleave("vector", "r", 1, 0, 0, HALF)
            interleave("vector", "r", 1, 1, 0, 288)
            interleave("scalar", "r", 1, 1, 288, HALF)
            quantize("r", 1, 0)
            for a in range(TILES):
                transpose_sums("00", a, row(a), ALL)
            interleave("scalar", "d", 1, 1, 160, HALF)
            quantize("r", 1, 1)
            multiply("01", "f0", "r1", [0, 1], ALL)
            interleave("vector", "d", 1, 1, 0, 160)
            subtract("00", 0, row(0), ALL)
            quantize("d", 1, 1)
            multiply("01", "G0", "d1", [1], ALL)
            for a in range(1, TILES):
                subtract("00", a, row(a), ALL)
            for a in range(TILES):
                weigh(gpsimd, "00", row(a), ALL)
            store("00", row(0), ALL)
            store("00", row(1), ALL)
            for a in range(TILES):
                unload("01", a)
                weigh(vector, "01", row(a), ALL)
                store("01", row(a), ALL)
            store("00", row(2), ALL)
            store("00", row(3), ALL)

            for stationary, moving in (("G1", "d1"), ("f1", "r1")):
                for a in range(2):
                    multiply("11", stationary, moving, [0, 1], row(a))
            multiply("11", "f1", "r1", [0, 1], row(2))
            multiply("11", "G1", "d1", [0, 1], row(2))
            for a in range(3):
                unload("11", a)
            transpose_sums("01", TILES, row(0), ALL)
            transpose_sums("11", 0, (0, 2), (0, 2))
            transpose_sums("01", TILES + 1, row(1), ALL)
            transpose_sums("01", TILES + 2, row(2), ALL)
            transpose_sums("11", 2, ALL, (2, 3))
            multiply("11", "G1", "d1", [0, 1], row(3))
            multiply("11", "f1", "r1", [0, 1], row(3))
            unload("11", 3)
            transpose_sums("01", TILES + 3, row(3), ALL)
            transpose_sums("11", 1, (2, 4), (0, 2))
            transpose_sums("11", 3, ALL, (3, 4))

            weigh(vector, "10", row(0), ALL)
            subtract("11", 0, (0, 2), (0, 2))
            weigh(gpsimd, "11", (0, 2), (0, 2))
            weigh(vector, "10", row(1), ALL)
            subtract("11", 2, (0, 3), (2, 3))
            weigh(gpsimd, "11", (0, 3), (2, 3))
            weigh(vector, "10", row(2), ALL)
            weigh(vector, "10", row(3), ALL)
            for a in range(TILES):
                store("10", row(a), ALL)
            store("11", (0, 2), (0, 3))
            subtract("11", 1, row(2), (0, 2))
            weigh(gpsimd, "11", row(2), (0, 2))
            store("11", row(2), (0, 3))
            subtract("11", 2, row(3), (2, 3), slot=3)
            subtract("11", 3, ALL, (3, 4))
            subtract("11", 1, row(3), (0, 2), slot=2)
            weigh(vector, "11", ALL, (3, 4))
            store("11", (0, 3), (3, 4))
            weigh(vector, "11", row(3), (0, 3))
            store("11", row(3), ALL)
